import numpy as np
import ml_dtypes


def mxq(x, axis, fmt="e4m3"):
    dtype, down = {"e4m3": (ml_dtypes.float8_e4m3fn, 7), "e5m2": (ml_dtypes.float8_e5m2, 14)}[fmt]
    v = np.moveaxis(np.asarray(x, np.float32).astype(ml_dtypes.bfloat16).astype(np.float64), axis, -1)
    blocks = v.reshape(v.shape[:-1] + (-1, 32))
    amax = np.abs(blocks).max(-1, keepdims=True)
    byte = np.maximum(np.where(amax > 0, np.frexp(amax)[1] - 1 + 127, 0) - down, 1)
    scale = np.exp2(byte - 127.0)
    codes = (blocks / scale).astype(np.float32).astype(dtype).astype(np.float64)
    return np.moveaxis((codes * scale).reshape(v.shape), -1, axis)


WIDE = False


def mx_kscale(k, group=512):
    if not WIDE:
        return np.ones(k)
    levels = np.array([10, -10, 5, -5, 0])
    if group != 512:
        return np.exp2(np.random.permutation(np.resize(levels, k // group))).repeat(group)
    if k % 512:
        return np.exp2(np.random.permutation(np.resize(levels, k // 32))).repeat(32)
    a = np.empty((k // 512, 16))
    for p in range(k // 512):
        a[p, :8] = np.random.permutation(np.resize(levels, 8))
        for g in range(8):
            far = levels[np.abs(levels - a[p, g]) >= 10]
            a[p, g + 8] = far[np.random.randint(len(far))]
    return np.exp2(a.ravel()).repeat(32)


def f64(x):
    return np.asarray(x).astype(np.float64)


H, D, N = 4, 256, 512


def setup_inputs():
    n = np.random.standard_normal
    s = mx_kscale(D, 0)[:, None]
    S = n((H, D, 128))
    S[:, :, 127] = np.random.uniform(0.5, 1.5, (H, D))
    return {
        "q": n((H, D, N)).astype(np.float32),
        "qa": (np.random.uniform(0.5, 2.0, (D, 1)) * s).astype(np.float32),
        "S": (S / s).astype(np.float32),
        "og": n((H, N, 128)).astype(np.float32),
    }


def reference(q, qa, S, og):
    fq = (1.0 / (1.0 + np.exp(-f64(q)))) * f64(qa)
    y = mxq(fq, 1, "e4m3").transpose(0, 2, 1) @ mxq(f64(S), 1, "e4m3")
    y = y / y[:, :, 127:128]
    y = y / (1.0 + np.exp(-f64(og)))
    return y

@@ -1,0 +1,247 @@
+from contextlib import ExitStack
+
+import concourse.mybir as mybir
+
+H, D, N, E = 4, 256, 512, 128
+FLOPS = 2 * H * N * D * E
+
+F32 = mybir.dt.float32
+BF16 = mybir.dt.bfloat16
+U32 = mybir.dt.uint32
+U8 = mybir.dt.uint8
+FP8X4 = mybir.dt.float8_e4m3fn_x4
+ACT = mybir.ActivationFunctionType
+ALU = mybir.AluOpType
+
+P = 128
+PACK = 4
+ROWS = D // PACK
+SIDE = P // ROWS
+R = 2
+W = P * R
+UNITS = [(g, n0) for g in range(H // SIDE) for n0 in range(0, N, W)]
+
+
+def tile_rows_read_sig_norm_gate_kernel(tc, q, qa, S, og, out):
+    nc = tc.nc
+    q_rows = q.rearrange("h d n -> (h d) n")
+    s_rows = S.rearrange("h d e -> (h d) e")
+
+    with ExitStack() as ctx:
+        sb = ctx.enter_context(tc.tile_pool(name="sb", bufs=1))
+        ps = ctx.enter_context(tc.psum_pool(name="ps", bufs=1))
+        ctx.enter_context(tc.manual_schedule())
+
+        warm_in = sb.tile([P, 1], F32, name="warm_in")
+        warm_out = sb.tile([P, 1], F32, name="warm_out")
+        qa_t = sb.tile([P, PACK], F32, name="qa_t")
+        qa_rows = qa.rearrange("(p j) o -> p (j o)", j=PACK)
+        for c in range(SIDE):
+            nc.scalar.dma_start(out=qa_t[ROWS * c : ROWS * (c + 1), :], in_=qa_rows)
+        nc.vector.memset(warm_in[:], 0.0)
+        nc.scalar.activation(out=warm_out[:], in_=warm_in[:], func=ACT.Sigmoid)
+
+        raw = {}
+        sig = {}
+        s_raw, s_bf, s_codes, s_scales = {}, {}, {}, {}
+        og_raw, gate, xb, codes, scales, acc, rec, res = {}, {}, {}, {}, {}, {}, {}, {}
+
+        def load_q(u, m0, m1):
+            g, n0 = UNITS[u]
+            t = sb.tile([P, PACK, R * (m1 - m0)], F32, name="raw_%d_%d" % (u, m0))
+            src = q_rows[P * PACK * g : P * PACK * (g + 1), n0 + R * m0 : n0 + R * m1]
+            nc.sync.dma_start(out=t[:], in_=src.rearrange("(p j) n -> p j n", j=PACK))
+            raw[u, m0] = (t, m0, m1)
+
+        def load_s(g):
+            s_raw[g] = sb.tile([P, PACK, E], F32, name="s_raw_%d" % g)
+            src = s_rows[P * PACK * g : P * PACK * (g + 1), :]
+            nc.sync.dma_start(out=s_raw[g][:], in_=src.rearrange("(p j) e -> p j e", j=PACK))
+
+        def unit_rows(t, u):
+            g, n0 = UNITS[u]
+            return t[SIDE * g : SIDE * (g + 1), n0 : n0 + W, :].rearrange("c (m r) e -> m c (r e)", r=R)
+
+        def load_og(u):
+            og_raw[u] = sb.tile([P, SIDE, R * E], F32, name="og_raw_%d" % u)
+            nc.sync.dma_start(out=og_raw[u][:], in_=unit_rows(og, u))
+
+        def new_sig(u, m0, m1):
+            sig[u, m0] = sb.tile([P, R, m1 - m0, PACK], F32, name="sig_%d_%d" % (u, m0))
+
+        def sigmoid_q(u, m0, m1, raw0, sig0):
+            t = raw[u, raw0][0]
+            src = t[:, :, R * (m0 - raw0) : R * (m1 - raw0)]
+            dst = sig[u, sig0][:, :, m0 - sig0 : m1 - sig0, :]
+            nc.scalar.activation(
+                out=dst.rearrange("p r m j -> p m j r"),
+                in_=src.rearrange("p j (m r) -> p m j r", r=R),
+                func=ACT.Sigmoid,
+            )
+
+        def sigmoid_og(u):
+            gate[u] = sb.tile([P, SIDE, R * E], F32, name="gate_%d" % u)
+            nc.scalar.activation(out=gate[u][:], in_=og_raw[u][:], func=ACT.Sigmoid)
+
+        def copy_s(g):
+            s_bf[g] = sb.tile([P, E, PACK], BF16, name="s_bf_%d" % g, align_bytes=64)
+            mover = nc.vector.tensor_copy if g == 0 else nc.scalar.copy
+            mover(
+                out=s_bf[g][:].rearrange("p (c i) j -> p c j i", i=4),
+                in_=s_raw[g][:].rearrange("p j (c i) -> p c j i", i=4),
+            )
+
+        def quant_s(g):
+            s_codes[g] = sb.tile([P, E], U32, name="s_codes_%d" % g, align_bytes=64)
+            s_scales[g] = sb.tile([P, E], U8, name="s_scales_%d" % g, align_bytes=64)
+            nc.vector.quantize_mx(
+                out=s_codes[g][:].bitcast(FP8X4),
+                scales=s_scales[g][:],
+                in_=s_bf[g][:].rearrange("p e j -> p (e j)"),
+            )
+
+        def new_xb(u):
+            xb[u] = sb.tile([P, R, P, PACK], BF16, name="xb_%d" % u, align_bytes=64)
+            codes[u] = sb.tile([P, R, P], U32, name="codes_%d" % u, align_bytes=64)
+            scales[u] = sb.tile([P, R, P], U8, name="scales_%d" % u, align_bytes=64)
+
+        def weigh_m(u, m0, m1):
+            nc.vector.tensor_tensor(
+                out=xb[u][:, :, m0:m1, :],
+                in0=sig[u, m0][:],
+                in1=qa_t[:].unsqueeze(1).unsqueeze(1).to_broadcast([P, R, m1 - m0, PACK]),
+                op=ALU.mult,
+            )
+
+        def weigh_r(u, r):
+            nc.vector.tensor_tensor(
+                out=xb[u][:, r, :, :],
+                in0=sig[u, 0][:, r, :, :],
+                in1=qa_t[:].unsqueeze(1).to_broadcast([P, P, PACK]),
+                op=ALU.mult,
+            )
+
+        def quant_q(u, r0, r1):
+            nc.vector.quantize_mx(
+                out=codes[u][:, r0:r1, :].rearrange("p r m -> p (r m)").bitcast(FP8X4),
+                scales=scales[u][:, r0:r1, :].rearrange("p r m -> p (r m)"),
+                in_=xb[u][:, r0:r1, :, :].rearrange("p r m j -> p (r m j)"),
+            )
+
+        def product(u, r):
+            g = UNITS[u][0]
+            for c in range(SIDE):
+                if (u, c) not in acc:
+                    acc[u, c] = ps.tile([P, R, E], F32, name="acc_%d_%d" % (u, c))
+                rows = slice(ROWS * c, ROWS * (c + 1))
+                nc.tensor.matmul_mx(
+                    out=acc[u, c][:, r, :],
+                    lhsT=codes[u][rows, r, :].bitcast(FP8X4),
+                    lhsT_scale=scales[u][rows, r, :],
+                    rhs=s_codes[g][rows, :].bitcast(FP8X4),
+                    rhs_scale=s_scales[g][rows, :],
+                    start=True,
+                    stop=True,
+                )
+
+        def inverse(u):
+            for c in range(SIDE):
+                rec[u, c] = sb.tile([P, R], F32, name="rec_%d_%d" % (u, c))
+                nc.vector.reciprocal(out=rec[u, c][:], in_=acc[u, c][:, :, E - 1])
+
+        def finish(u, c, r):
+            if u not in res:
+                res[u] = sb.tile([P, SIDE, R * E], F32, name="res_%d" % u)
+            cols = slice(E * r, E * (r + 1))
+            nc.vector.scalar_tensor_tensor(
+                out=res[u][:, c, cols],
+                in0=acc[u, c][:, r, :],
+                scalar=rec[u, c][:, r : r + 1],
+                in1=gate[u][:, c, cols],
+                op0=ALU.mult,
+                op1=ALU.mult,
+            )
+
+        def store(u, c0, c1):
+            nc.sync.dma_start(out=unit_rows(out, u)[:, c0:c1, :], in_=res[u][:, c0:c1, :])
+
+        HALF = P // 2
+        load_q(0, 0, HALF)
+        load_s(0)
+        load_q(0, HALF, P)
+        load_q(1, 0, P)
+        load_og(0)
+        load_s(1)
+        load_q(2, 0, P)
+        load_og(1)
+        load_q(3, 0, P)
+        load_og(2)
+        load_og(3)
+
+        def sig_half(u, m0, raw0):
+            new_sig(u, m0, m0 + HALF)
+            sigmoid_q(u, m0, m0 + HALF, raw0, m0)
+
+        sig_half(0, 0, 0)
+        sig_half(0, HALF, HALF)
+        sig_half(1, 0, 0)
+        sig_half(1, HALF, 0)
+        sigmoid_og(0)
+        copy_s(1)
+        sig_half(2, 0, 0)
+        sig_half(2, HALF, 0)
+        sigmoid_og(1)
+        new_sig(3, 0, P)
+        sigmoid_q(3, 0, P, 0, 0)
+        sigmoid_og(2)
+        sigmoid_og(3)
+
+        for u in range(4):
+            new_xb(u)
+
+        def products(u):
+            for r in range(R):
+                product(u, r)
+
+        def finish_all(u):
+            for c in range(SIDE):
+                for r in range(R):
+                    finish(u, c, r)
+            store(u, 0, SIDE)
+
+        copy_s(0)
+        weigh_m(0, 0, HALF)
+        quant_s(0)
+        weigh_m(0, HALF, P)
+        quant_q(0, 0, R)
+        products(0)
+        weigh_m(1, 0, HALF)
+        inverse(0)
+        weigh_m(1, HALF, P)
+        finish_all(0)
+        quant_q(1, 0, R)
+        products(1)
+        quant_s(1)
+        weigh_m(2, 0, HALF)
+        inverse(1)
+        weigh_m(2, HALF, P)
+        finish_all(1)
+        quant_q(2, 0, R)
+        products(2)
+        weigh_r(3, 0)
+        weigh_r(3, 1)
+        quant_q(3, 0, 1)
+        product(3, 0)
+        inverse(2)
+        quant_q(3, 1, 2)
+        product(3, 1)
+        finish(2, 0, 0)
+        finish(2, 0, 1)
+        finish(2, 1, 0)
+        inverse(3)
+        finish(2, 1, 1)
+        store(2, 0, SIDE)
+        for c in range(SIDE):
+            for r in range(R):
+                finish(3, c, r)
+            store(3, c, c + 1)

@@ -166,82 +166,58 @@ def tile_rows_read_sig_norm_gate_kernel(tc, q, qa, S, og, out):
             nc.sync.dma_start(out=unit_rows(out, u)[:, c0:c1, :], in_=res[u][:, c0:c1, :])
 
         HALF = P // 2
-        load_q(0, 0, HALF)
+        load_q(0, 0, P)
         load_s(0)
-        load_q(0, HALF, P)
-        load_q(1, 0, P)
-        load_og(0)
+        for u in (1, 2, 3):
+            load_q(u, 0, P)
         load_s(1)
-        load_q(2, 0, P)
-        load_og(1)
-        load_q(3, 0, P)
-        load_og(2)
-        load_og(3)
-
-        def sig_half(u, m0, raw0):
-            new_sig(u, m0, m0 + HALF)
-            sigmoid_q(u, m0, m0 + HALF, raw0, m0)
-
-        sig_half(0, 0, 0)
-        sig_half(0, HALF, HALF)
-        sig_half(1, 0, 0)
-        sig_half(1, HALF, 0)
-        sigmoid_og(0)
-        copy_s(1)
-        sig_half(2, 0, 0)
-        sig_half(2, HALF, 0)
-        sigmoid_og(1)
-        new_sig(3, 0, P)
-        sigmoid_q(3, 0, P, 0, 0)
-        sigmoid_og(2)
-        sigmoid_og(3)
+        for u in range(4):
+            load_og(u)
 
         for u in range(4):
             new_xb(u)
+            for m0 in (0, HALF):
+                new_sig(u, m0, m0 + HALF)
+                sigmoid_q(u, m0, m0 + HALF, 0, m0)
+        copy_s(1)
+        for u in range(4):
+            sigmoid_og(u)
 
-        def products(u):
+        def quant_mul(u):
+            quant_q(u, 0, R)
             for r in range(R):
                 product(u, r)
 
-        def finish_all(u):
-            for c in range(SIDE):
-                for r in range(R):
-                    finish(u, c, r)
-            store(u, 0, SIDE)
+        def finish_head(u, c):
+            for r in range(R):
+                finish(u, c, r)
+            store(u, c, c + 1)
 
         copy_s(0)
         weigh_m(0, 0, HALF)
-        quant_s(0)
         weigh_m(0, HALF, P)
-        quant_q(0, 0, R)
-        products(0)
+        quant_s(0)
+        quant_mul(0)
         weigh_m(1, 0, HALF)
-        inverse(0)
         weigh_m(1, HALF, P)
-        finish_all(0)
-        quant_q(1, 0, R)
-        products(1)
-        quant_s(1)
+        inverse(0)
         weigh_m(2, 0, HALF)
-        inverse(1)
+        quant_mul(1)
         weigh_m(2, HALF, P)
-        finish_all(1)
+        weigh_m(3, 0, HALF)
+        inverse(1)
         quant_q(2, 0, R)
-        products(2)
-        weigh_r(3, 0)
-        weigh_r(3, 1)
-        quant_q(3, 0, 1)
-        product(3, 0)
+        weigh_m(3, HALF, P)
+        quant_s(1)
+        for r in range(R):
+            product(2, r)
+        quant_mul(3)
+        finish_head(0, 0)
+        finish_head(0, 1)
         inverse(2)
-        quant_q(3, 1, 2)
-        product(3, 1)
-        finish(2, 0, 0)
-        finish(2, 0, 1)
-        finish(2, 1, 0)
+        finish_head(1, 0)
+        finish_head(1, 1)
         inverse(3)
-        finish(2, 1, 1)
-        store(2, 0, SIDE)
-        for c in range(SIDE):
-            for r in range(R):
-                finish(3, c, r)
-            store(3, c, c + 1)
+        for u in (2, 3):
+            for c in range(SIDE):
+                finish_head(u, c)

@@ -67,15 +67,14 @@ def tile_rows_read_sig_norm_gate_kernel(tc, q, qa, S, og, out):
             nc.sync.dma_start(out=og_raw[u][:], in_=unit_rows(og, u))
 
         def new_sig(u, m0, m1):
-            sig[u, m0] = sb.tile([P, R, m1 - m0, PACK], F32, name="sig_%d_%d" % (u, m0))
+            sig[u, m0] = sb.tile([P, 2, R * (m1 - m0), 2], F32, name="sig_%d_%d" % (u, m0))
 
         def sigmoid_q(u, m0, m1, raw0, sig0):
             t = raw[u, raw0][0]
             src = t[:, :, R * (m0 - raw0) : R * (m1 - raw0)]
-            dst = sig[u, sig0][:, :, m0 - sig0 : m1 - sig0, :]
             nc.scalar.activation(
-                out=dst.rearrange("p r m j -> p m j r"),
-                in_=src.rearrange("p j (m r) -> p m j r", r=R),
+                out=sig[u, sig0][:],
+                in_=src.rearrange("p (a b) n -> p a n b", b=2),
                 func=ACT.Sigmoid,
             )
 
@@ -107,17 +106,9 @@ def tile_rows_read_sig_norm_gate_kernel(tc, q, qa, S, og, out):
 
         def weigh_m(u, m0, m1):
             nc.vector.tensor_tensor(
-                out=xb[u][:, :, m0:m1, :],
-                in0=sig[u, m0][:],
-                in1=qa_t[:].unsqueeze(1).unsqueeze(1).to_broadcast([P, R, m1 - m0, PACK]),
-                op=ALU.mult,
-            )
-
-        def weigh_r(u, r):
-            nc.vector.tensor_tensor(
-                out=xb[u][:, r, :, :],
-                in0=sig[u, 0][:, r, :, :],
-                in1=qa_t[:].unsqueeze(1).to_broadcast([P, P, PACK]),
+                out=xb[u][:, :, m0:m1, :].rearrange("p r m (a b) -> p m r a b", b=2),
+                in0=sig[u, m0][:].rearrange("p a (m r) b -> p m r a b", r=R),
+                in1=qa_t[:].rearrange("p (a b) -> p a b", b=2).unsqueeze(1).unsqueeze(1).to_broadcast([P, m1 - m0, R, 2, 2]),
                 op=ALU.mult,
             )
 
@@ -131,11 +122,11 @@ def tile_rows_read_sig_norm_gate_kernel(tc, q, qa, S, og, out):
         def product(u, r):
             g = UNITS[u][0]
             for c in range(SIDE):
-                if (u, c) not in acc:
-                    acc[u, c] = ps.tile([P, R, E], F32, name="acc_%d_%d" % (u, c))
+                if (g, c) not in acc:
+                    acc[g, c] = ps.tile([P, 2 * R, E], F32, name="acc_%d_%d" % (g, c))
                 rows = slice(ROWS * c, ROWS * (c + 1))
                 nc.tensor.matmul_mx(
-                    out=acc[u, c][:, r, :],
+                    out=acc[g, c][:, R * (u % 2) + r, :],
                     lhsT=codes[u][rows, r, :].bitcast(FP8X4),
                     lhsT_scale=scales[u][rows, r, :],
                     rhs=s_codes[g][rows, :].bitcast(FP8X4),
@@ -144,19 +135,21 @@ def tile_rows_read_sig_norm_gate_kernel(tc, q, qa, S, og, out):
                     stop=True,
                 )
 
-        def inverse(u):
+        def inverse(g):
             for c in range(SIDE):
-                rec[u, c] = sb.tile([P, R], F32, name="rec_%d_%d" % (u, c))
-                nc.vector.reciprocal(out=rec[u, c][:], in_=acc[u, c][:, :, E - 1])
+                rec[g, c] = sb.tile([P, 2 * R], F32, name="rec_%d_%d" % (g, c))
+                nc.vector.reciprocal(out=rec[g, c][:], in_=acc[g, c][:, :, E - 1])
 
         def finish(u, c, r):
             if u not in res:
                 res[u] = sb.tile([P, SIDE, R * E], F32, name="res_%d" % u)
             cols = slice(E * r, E * (r + 1))
+            g = UNITS[u][0]
+            t = R * (u % 2) + r
             nc.vector.scalar_tensor_tensor(
                 out=res[u][:, c, cols],
-                in0=acc[u, c][:, r, :],
-                scalar=rec[u, c][:, r : r + 1],
+                in0=acc[g, c][:, t, :],
+                scalar=rec[g, c][:, t : t + 1],
                 in1=gate[u][:, c, cols],
                 op0=ALU.mult,
                 op1=ALU.mult,
@@ -168,8 +161,9 @@ def tile_rows_read_sig_norm_gate_kernel(tc, q, qa, S, og, out):
         HALF = P // 2
         load_q(0, 0, P)
         load_s(0)
-        for u in (1, 2, 3):
-            load_q(u, 0, P)
+        load_q(1, 0, P)
+        load_q(2, 0, P)
+        load_q(3, 0, P)
         load_s(1)
         for u in range(4):
             load_og(u)
@@ -183,8 +177,7 @@ def tile_rows_read_sig_norm_gate_kernel(tc, q, qa, S, og, out):
         for u in range(4):
             sigmoid_og(u)
 
-        def quant_mul(u):
-            quant_q(u, 0, R)
+        def products(u):
             for r in range(R):
                 product(u, r)
 
@@ -197,27 +190,27 @@ def tile_rows_read_sig_norm_gate_kernel(tc, q, qa, S, og, out):
         weigh_m(0, 0, HALF)
         weigh_m(0, HALF, P)
         quant_s(0)
-        quant_mul(0)
+        quant_q(0, 0, R)
+        products(0)
         weigh_m(1, 0, HALF)
         weigh_m(1, HALF, P)
-        inverse(0)
         weigh_m(2, 0, HALF)
-        quant_mul(1)
+        quant_q(1, 0, R)
+        products(1)
         weigh_m(2, HALF, P)
         weigh_m(3, 0, HALF)
-        inverse(1)
         quant_q(2, 0, R)
         weigh_m(3, HALF, P)
+        inverse(0)
         quant_s(1)
-        for r in range(R):
-            product(2, r)
-        quant_mul(3)
+        products(2)
+        quant_q(3, 0, R)
+        products(3)
         finish_head(0, 0)
         finish_head(0, 1)
-        inverse(2)
         finish_head(1, 0)
+        inverse(1)
         finish_head(1, 1)
-        inverse(3)
         for u in (2, 3):
             for c in range(SIDE):
                 finish_head(u, c)

@@ -32,14 +32,8 @@ def tile_rows_read_sig_norm_gate_kernel(tc, q, qa, S, og, out):
         ps = ctx.enter_context(tc.psum_pool(name="ps", bufs=1))
         ctx.enter_context(tc.manual_schedule())
 
-        warm_in = sb.tile([P, 1], F32, name="warm_in")
-        warm_out = sb.tile([P, 1], F32, name="warm_out")
         qa_t = sb.tile([P, PACK], F32, name="qa_t")
         qa_rows = qa.rearrange("(p j) o -> p (j o)", j=PACK)
-        for c in range(SIDE):
-            nc.scalar.dma_start(out=qa_t[ROWS * c : ROWS * (c + 1), :], in_=qa_rows)
-        nc.vector.memset(warm_in[:], 0.0)
-        nc.scalar.activation(out=warm_out[:], in_=warm_in[:], func=ACT.Sigmoid)
 
         raw = {}
         sig = {}
@@ -52,6 +46,23 @@ def tile_rows_read_sig_norm_gate_kernel(tc, q, qa, S, og, out):
             src = q_rows[P * PACK * g : P * PACK * (g + 1), n0 + R * m0 : n0 + R * m1]
             nc.sync.dma_start(out=t[:], in_=src.rearrange("(p j) n -> p j n", j=PACK))
             raw[u, m0] = (t, m0, m1)
+
+        def load_qa_pair(u, a):
+            g, n0 = UNITS[u]
+            t = sb.tile([P, 2, W], F32, name="rawa_%d_%d" % (u, a))
+            src = q_rows[P * PACK * g : P * PACK * (g + 1), n0 : n0 + W]
+            nc.sync.dma_start(out=t[:], in_=src.rearrange("(p a b) n -> p a b n", a=2, b=2)[:, a, :, :])
+            raw[u, "a", a] = t
+
+        def sigmoid_pair(u, a, m0, m1):
+            if (u, "all") not in sig:
+                new_xb(u)
+                sig[u, "all"] = sb.tile([P, 2, W, 2], F32, name="sigall_%d" % u)
+            nc.scalar.activation(
+                out=sig[u, "all"][:, a, R * m0 : R * m1, :],
+                in_=raw[u, "a", a][:, :, R * m0 : R * m1].rearrange("p b n -> p n b"),
+                func=ACT.Sigmoid,
+            )
 
         def load_s(g):
             s_raw[g] = sb.tile([P, PACK, E], F32, name="s_raw_%d" % g)
@@ -84,8 +95,7 @@ def tile_rows_read_sig_norm_gate_kernel(tc, q, qa, S, og, out):
 
         def copy_s(g):
             s_bf[g] = sb.tile([P, E, PACK], BF16, name="s_bf_%d" % g, align_bytes=64)
-            mover = nc.vector.tensor_copy if g == 0 else nc.scalar.copy
-            mover(
+            nc.scalar.copy(
                 out=s_bf[g][:].rearrange("p (c i) j -> p c j i", i=4),
                 in_=s_raw[g][:].rearrange("p j (c i) -> p c j i", i=4),
             )
@@ -105,9 +115,13 @@ def tile_rows_read_sig_norm_gate_kernel(tc, q, qa, S, og, out):
             scales[u] = sb.tile([P, R, P], U8, name="scales_%d" % u, align_bytes=64)
 
         def weigh_m(u, m0, m1):
+            if (u, "all") in sig:
+                src = sig[u, "all"][:, :, R * m0 : R * m1, :]
+            else:
+                src = sig[u, m0][:]
             nc.vector.tensor_tensor(
                 out=xb[u][:, :, m0:m1, :].rearrange("p r m (a b) -> p m r a b", b=2),
-                in0=sig[u, m0][:].rearrange("p a (m r) b -> p m r a b", r=R),
+                in0=src.rearrange("p a (m r) b -> p m r a b", r=R),
                 in1=qa_t[:].rearrange("p (a b) -> p a b", b=2).unsqueeze(1).unsqueeze(1).to_broadcast([P, m1 - m0, R, 2, 2]),
                 op=ALU.mult,
             )
@@ -158,25 +172,6 @@ def tile_rows_read_sig_norm_gate_kernel(tc, q, qa, S, og, out):
         def store(u, c0, c1):
             nc.sync.dma_start(out=unit_rows(out, u)[:, c0:c1, :], in_=res[u][:, c0:c1, :])
 
-        HALF = P // 2
-        load_q(0, 0, P)
-        load_s(0)
-        load_q(1, 0, P)
-        load_q(2, 0, P)
-        load_q(3, 0, P)
-        load_s(1)
-        for u in range(4):
-            load_og(u)
-
-        for u in range(4):
-            new_xb(u)
-            for m0 in (0, HALF):
-                new_sig(u, m0, m0 + HALF)
-                sigmoid_q(u, m0, m0 + HALF, 0, m0)
-        copy_s(1)
-        for u in range(4):
-            sigmoid_og(u)
-
         def products(u):
             for r in range(R):
                 product(u, r)
@@ -186,31 +181,66 @@ def tile_rows_read_sig_norm_gate_kernel(tc, q, qa, S, og, out):
                 finish(u, c, r)
             store(u, c, c + 1)
 
+        def sigmoid_unit(u, cuts, piece):
+            new_xb(u)
+            for m0, m1 in zip(cuts, cuts[1:]):
+                new_sig(u, m0, m1)
+                sigmoid_q(u, m0, m1, m0 - m0 % piece, m0)
+
+        HALF = P // 2
+        QUARTER = P // 4
+        load_q(0, 0, HALF)
+        for c in range(SIDE):
+            nc.sync.dma_start(out=qa_t[ROWS * c : ROWS * (c + 1), :], in_=qa_rows)
+        load_q(0, HALF, P)
+        for u in (1, 2):
+            for a in range(2):
+                load_qa_pair(u, a)
+        load_s(0)
+        for a in range(2):
+            load_qa_pair(3, a)
+        load_s(1)
+        for u in range(4):
+            load_og(u)
+
+        def sigmoid_by_pairs(u):
+            sigmoid_pair(u, 0, 0, P)
+            sigmoid_pair(u, 1, 0, HALF)
+            sigmoid_pair(u, 1, HALF, P)
+
+        sigmoid_unit(0, (0, QUARTER, HALF, HALF + QUARTER, P), HALF)
+        sigmoid_by_pairs(1)
+        sigmoid_by_pairs(2)
         copy_s(0)
-        weigh_m(0, 0, HALF)
-        weigh_m(0, HALF, P)
-        quant_s(0)
+        sigmoid_by_pairs(3)
+        copy_s(1)
+        for u in range(4):
+            sigmoid_og(u)
+
+        for m0 in range(0, P, QUARTER):
+            weigh_m(0, m0, m0 + QUARTER)
         quant_q(0, 0, R)
-        products(0)
         weigh_m(1, 0, HALF)
         weigh_m(1, HALF, P)
         weigh_m(2, 0, HALF)
         quant_q(1, 0, R)
-        products(1)
         weigh_m(2, HALF, P)
-        weigh_m(3, 0, HALF)
+        quant_s(0)
+        products(0)
+        products(1)
         quant_q(2, 0, R)
+        weigh_m(3, 0, HALF)
         weigh_m(3, HALF, P)
-        inverse(0)
         quant_s(1)
         products(2)
+        inverse(0)
         quant_q(3, 0, R)
         products(3)
         finish_head(0, 0)
         finish_head(0, 1)
         finish_head(1, 0)
-        inverse(1)
         finish_head(1, 1)
+        inverse(1)
         for u in (2, 3):
             for c in range(SIDE):
                 finish_head(u, c)

@@ -73,9 +73,12 @@ def tile_rows_read_sig_norm_gate_kernel(tc, q, qa, S, og, out):
             g, n0 = UNITS[u]
             return t[SIDE * g : SIDE * (g + 1), n0 : n0 + W, :].rearrange("c (m r) e -> m c (r e)", r=R)
 
-        def load_og(u):
-            og_raw[u] = sb.tile([P, SIDE, R * E], F32, name="og_raw_%d" % u)
-            nc.sync.dma_start(out=og_raw[u][:], in_=unit_rows(og, u))
+        def head_rows(t, h):
+            return t[h].rearrange("(k m r) e -> m k (r e)", r=R, m=P)
+
+        def load_og(h):
+            og_raw[h] = sb.tile([P, 2, R * E], F32, name="og_raw_%d" % h)
+            nc.sync.dma_start(out=og_raw[h][:], in_=head_rows(og, h))
 
         def new_sig(u, m0, m1):
             sig[u, m0] = sb.tile([P, 2, R * (m1 - m0), 2], F32, name="sig_%d_%d" % (u, m0))
@@ -89,9 +92,11 @@ def tile_rows_read_sig_norm_gate_kernel(tc, q, qa, S, og, out):
                 func=ACT.Sigmoid,
             )
 
-        def sigmoid_og(u):
-            gate[u] = sb.tile([P, SIDE, R * E], F32, name="gate_%d" % u)
-            nc.scalar.activation(out=gate[u][:], in_=og_raw[u][:], func=ACT.Sigmoid)
+        def sigmoid_og(h, k0, k1):
+            t = sb.tile([P, k1 - k0, R * E], F32, name="gate_%d_%d" % (h, k0))
+            nc.scalar.activation(out=t[:], in_=og_raw[h][:, k0:k1, :], func=ACT.Sigmoid)
+            for k in range(k0, k1):
+                gate[h, k] = t[:, k - k0, :]
 
         def copy_s(g):
             s_bf[g] = sb.tile([P, E, PACK], BF16, name="s_bf_%d" % g, align_bytes=64)
@@ -149,37 +154,47 @@ def tile_rows_read_sig_norm_gate_kernel(tc, q, qa, S, og, out):
                     stop=True,
                 )
 
-        def inverse(g):
-            for c in range(SIDE):
-                rec[g, c] = sb.tile([P, 2 * R], F32, name="rec_%d_%d" % (g, c))
-                nc.vector.reciprocal(out=rec[g, c][:], in_=acc[g, c][:, :, E - 1])
+        def inverse(h):
+            g, c = divmod(h, SIDE)
+            rec[g, c] = sb.tile([P, 2 * R], F32, name="rec_%d_%d" % (g, c))
+            nc.vector.reciprocal(out=rec[g, c][:], in_=acc[g, c][:, :, E - 1])
 
-        def finish(u, c, r):
-            if u not in res:
-                res[u] = sb.tile([P, SIDE, R * E], F32, name="res_%d" % u)
-            cols = slice(E * r, E * (r + 1))
-            g = UNITS[u][0]
-            t = R * (u % 2) + r
-            nc.vector.scalar_tensor_tensor(
-                out=res[u][:, c, cols],
-                in0=acc[g, c][:, t, :],
-                scalar=rec[g, c][:, t : t + 1],
-                in1=gate[u][:, c, cols],
-                op0=ALU.mult,
-                op1=ALU.mult,
-            )
+        def finish(h, k, r0=0, r1=R):
+            g, c = divmod(h, SIDE)
+            t_out = sb.tile([P, (r1 - r0) * E], F32, name="res_%d_%d_%d" % (h, k, r0))
+            for r in range(r0, r1):
+                cols = slice(E * r, E * (r + 1))
+                t = R * k + r
+                nc.vector.scalar_tensor_tensor(
+                    out=t_out[:, E * (r - r0) : E * (r - r0 + 1)],
+                    in0=acc[g, c][:, t, :],
+                    scalar=rec[g, c][:, t : t + 1],
+                    in1=gate[h, k][:, cols],
+                    op0=ALU.mult,
+                    op1=ALU.mult,
+                )
+            nc.sync.dma_start(out=head_rows(out, h)[:, k, E * r0 : E * r1], in_=t_out[:])
 
-        def store(u, c0, c1):
-            nc.sync.dma_start(out=unit_rows(out, u)[:, c0:c1, :], in_=res[u][:, c0:c1, :])
+        def normalise(h, k):
+            g, c = divmod(h, SIDE)
+            res[h, k] = sb.tile([P, R * E], F32, name="part_%d_%d" % (h, k))
+            for r in range(R):
+                t = R * k + r
+                nc.scalar.activation(
+                    out=res[h, k][:, E * r : E * (r + 1)], in_=acc[g, c][:, t, :], func=ACT.Copy, scale=rec[g, c][:, t : t + 1]
+                )
+
+        def gate_aside(h, k):
+            t_out = sb.tile([P, R * E], F32, name="res_%d_%d" % (h, k))
+            nc.gpsimd.tensor_tensor(out=t_out[:], in0=res[h, k][:], in1=gate[h, k], op=ALU.mult)
+            return t_out
+
+        def store_aside(h, k, t_out):
+            nc.sync.dma_start(out=head_rows(out, h)[:, k, :], in_=t_out[:])
 
         def products(u):
             for r in range(R):
                 product(u, r)
-
-        def finish_head(u, c):
-            for r in range(R):
-                finish(u, c, r)
-            store(u, c, c + 1)
 
         def sigmoid_unit(u, cuts, piece):
             new_xb(u)
@@ -189,36 +204,41 @@ def tile_rows_read_sig_norm_gate_kernel(tc, q, qa, S, og, out):
 
         HALF = P // 2
         QUARTER = P // 4
-        load_q(0, 0, HALF)
-        for c in range(SIDE):
-            nc.sync.dma_start(out=qa_t[ROWS * c : ROWS * (c + 1), :], in_=qa_rows)
-        load_q(0, HALF, P)
-        for u in (1, 2):
-            for a in range(2):
-                load_qa_pair(u, a)
-        load_s(0)
-        for a in range(2):
-            load_qa_pair(3, a)
-        load_s(1)
-        for u in range(4):
-            load_og(u)
-
         def sigmoid_by_pairs(u):
             sigmoid_pair(u, 0, 0, P)
             sigmoid_pair(u, 1, 0, HALF)
             sigmoid_pair(u, 1, HALF, P)
 
-        sigmoid_unit(0, (0, QUARTER, HALF, HALF + QUARTER, P), HALF)
+        load_qa_pair(0, 0)
+        for c in range(SIDE):
+            nc.sync.dma_start(out=qa_t[ROWS * c : ROWS * (c + 1), :], in_=qa_rows)
+        load_qa_pair(0, 1)
+        load_qa_pair(1, 0)
+        load_qa_pair(1, 1)
+        load_qa_pair(2, 0)
+        load_qa_pair(2, 1)
+        load_s(0)
+        load_qa_pair(3, 0)
+        load_qa_pair(3, 1)
+        load_s(1)
+        load_og(0)
+        load_og(1)
+        load_og(2)
+        load_og(3)
+
+        sigmoid_by_pairs(0)
         sigmoid_by_pairs(1)
         sigmoid_by_pairs(2)
         copy_s(0)
         sigmoid_by_pairs(3)
         copy_s(1)
-        for u in range(4):
-            sigmoid_og(u)
+        sigmoid_og(0, 0, 2)
+        sigmoid_og(1, 0, 2)
+        sigmoid_og(2, 0, 2)
+        sigmoid_og(3, 0, 2)
 
-        for m0 in range(0, P, QUARTER):
-            weigh_m(0, m0, m0 + QUARTER)
+        weigh_m(0, 0, HALF)
+        weigh_m(0, HALF, P)
         quant_q(0, 0, R)
         weigh_m(1, 0, HALF)
         weigh_m(1, HALF, P)
@@ -234,13 +254,18 @@ def tile_rows_read_sig_norm_gate_kernel(tc, q, qa, S, og, out):
         quant_s(1)
         products(2)
         inverse(0)
-        quant_q(3, 0, R)
-        products(3)
-        finish_head(0, 0)
-        finish_head(0, 1)
-        finish_head(1, 0)
-        finish_head(1, 1)
         inverse(1)
-        for u in (2, 3):
-            for c in range(SIDE):
-                finish_head(u, c)
+        quant_q(3, 0, 1)
+        product(3, 0)
+        quant_q(3, 1, 2)
+        product(3, 1)
+        finish(0, 0)
+        finish(0, 1)
+        finish(1, 0)
+        finish(1, 1)
+        inverse(2)
+        inverse(3)
+        finish(2, 0)
+        finish(2, 1)
+        finish(3, 0)
+        finish(3, 1)

@@ -234,8 +234,6 @@ def tile_rows_read_sig_norm_gate_kernel(tc, q, qa, S, og, out):
         copy_s(1)
         sigmoid_og(0, 0, 2)
         sigmoid_og(1, 0, 2)
-        sigmoid_og(2, 0, 2)
-        sigmoid_og(3, 0, 2)
 
         weigh_m(0, 0, HALF)
         weigh_m(0, HALF, P)
@@ -259,12 +257,16 @@ def tile_rows_read_sig_norm_gate_kernel(tc, q, qa, S, og, out):
         product(3, 0)
         quant_q(3, 1, 2)
         product(3, 1)
+        normalise(1, 0)
+        aside_10 = gate_aside(1, 0)
+        sigmoid_og(2, 0, 2)
+        sigmoid_og(3, 0, 2)
         finish(0, 0)
         finish(0, 1)
-        finish(1, 0)
         finish(1, 1)
         inverse(2)
         inverse(3)
+        store_aside(1, 0, aside_10)
         finish(2, 0)
         finish(2, 1)
         finish(3, 0)

@@ -19,13 +19,18 @@ ROWS = D // PACK
 SIDE = P // ROWS
 R = 2
 W = P * R
-UNITS = [(g, n0) for g in range(H // SIDE) for n0 in range(0, N, W)]
+K = N // W
+HALVES = ((0, P // 2), (P // 2, P))
 
 
 def tile_rows_read_sig_norm_gate_kernel(tc, q, qa, S, og, out):
     nc = tc.nc
-    q_rows = q.rearrange("h d n -> (h d) n")
-    s_rows = S.rearrange("h d e -> (h d) e")
+    q_rows = q.rearrange("h (p a b) n -> (h p) a b n", a=2, b=2)
+    s_rows = S.rearrange("h (p j) e -> (h p) j e", j=PACK)
+    qa_rows = qa.rearrange("(p j) o -> p (j o)", j=PACK)
+
+    def head_rows(t, h):
+        return t[h].rearrange("(k m r) e -> m k (r e)", r=R, m=P)
 
     with ExitStack() as ctx:
         sb = ctx.enter_context(tc.tile_pool(name="sb", bufs=1))
@@ -33,72 +38,42 @@ def tile_rows_read_sig_norm_gate_kernel(tc, q, qa, S, og, out):
         ctx.enter_context(tc.manual_schedule())
 
         qa_t = sb.tile([P, PACK], F32, name="qa_t")
-        qa_rows = qa.rearrange("(p j) o -> p (j o)", j=PACK)
-
-        raw = {}
-        sig = {}
+        q_raw, phi, q_bf, q_codes, q_scales = {}, {}, {}, {}, {}
         s_raw, s_bf, s_codes, s_scales = {}, {}, {}, {}
-        og_raw, gate, xb, codes, scales, acc, rec, res = {}, {}, {}, {}, {}, {}, {}, {}
+        og_raw, gate, acc, rec = {}, {}, {}, {}
 
-        def load_q(u, m0, m1):
-            g, n0 = UNITS[u]
-            t = sb.tile([P, PACK, R * (m1 - m0)], F32, name="raw_%d_%d" % (u, m0))
-            src = q_rows[P * PACK * g : P * PACK * (g + 1), n0 + R * m0 : n0 + R * m1]
-            nc.sync.dma_start(out=t[:], in_=src.rearrange("(p j) n -> p j n", j=PACK))
-            raw[u, m0] = (t, m0, m1)
+        def load_q(u):
+            g, k = divmod(u, K)
+            for a in range(2):
+                q_raw[u, a] = sb.tile([P, 2, W], F32, name="q_raw_%d_%d" % (u, a))
+                nc.sync.dma_start(out=q_raw[u, a][:], in_=q_rows[P * g : P * (g + 1), a, :, W * k : W * (k + 1)])
 
-        def load_qa_pair(u, a):
-            g, n0 = UNITS[u]
-            t = sb.tile([P, 2, W], F32, name="rawa_%d_%d" % (u, a))
-            src = q_rows[P * PACK * g : P * PACK * (g + 1), n0 : n0 + W]
-            nc.sync.dma_start(out=t[:], in_=src.rearrange("(p a b) n -> p a b n", a=2, b=2)[:, a, :, :])
-            raw[u, "a", a] = t
-
-        def sigmoid_pair(u, a, m0, m1):
-            if (u, "all") not in sig:
-                new_xb(u)
-                sig[u, "all"] = sb.tile([P, 2, W, 2], F32, name="sigall_%d" % u)
-            nc.scalar.activation(
-                out=sig[u, "all"][:, a, R * m0 : R * m1, :],
-                in_=raw[u, "a", a][:, :, R * m0 : R * m1].rearrange("p b n -> p n b"),
-                func=ACT.Sigmoid,
-            )
+        def load_qa():
+            for c in range(SIDE):
+                nc.sync.dma_start(out=qa_t[ROWS * c : ROWS * (c + 1), :], in_=qa_rows)
 
         def load_s(g):
             s_raw[g] = sb.tile([P, PACK, E], F32, name="s_raw_%d" % g)
-            src = s_rows[P * PACK * g : P * PACK * (g + 1), :]
-            nc.sync.dma_start(out=s_raw[g][:], in_=src.rearrange("(p j) e -> p j e", j=PACK))
-
-        def unit_rows(t, u):
-            g, n0 = UNITS[u]
-            return t[SIDE * g : SIDE * (g + 1), n0 : n0 + W, :].rearrange("c (m r) e -> m c (r e)", r=R)
-
-        def head_rows(t, h):
-            return t[h].rearrange("(k m r) e -> m k (r e)", r=R, m=P)
+            nc.sync.dma_start(out=s_raw[g][:], in_=s_rows[P * g : P * (g + 1), :, :])
 
         def load_og(h):
-            og_raw[h] = sb.tile([P, 2, R * E], F32, name="og_raw_%d" % h)
+            og_raw[h] = sb.tile([P, K, R * E], F32, name="og_raw_%d" % h)
             nc.sync.dma_start(out=og_raw[h][:], in_=head_rows(og, h))
 
-        def new_sig(u, m0, m1):
-            sig[u, m0] = sb.tile([P, 2, R * (m1 - m0), 2], F32, name="sig_%d_%d" % (u, m0))
+        def sigmoid_q(u):
+            phi[u] = sb.tile([P, 2, W, 2], F32, name="phi_%d" % u)
+            for a, (m0, m1) in [(0, (0, P))] + [(1, half) for half in HALVES]:
+                nc.scalar.activation(
+                    out=phi[u][:, a, R * m0 : R * m1, :],
+                    in_=q_raw[u, a][:, :, R * m0 : R * m1].rearrange("p b n -> p n b"),
+                    func=ACT.Sigmoid,
+                )
 
-        def sigmoid_q(u, m0, m1, raw0, sig0):
-            t = raw[u, raw0][0]
-            src = t[:, :, R * (m0 - raw0) : R * (m1 - raw0)]
-            nc.scalar.activation(
-                out=sig[u, sig0][:],
-                in_=src.rearrange("p (a b) n -> p a n b", b=2),
-                func=ACT.Sigmoid,
-            )
+        def sigmoid_og(h):
+            gate[h] = sb.tile([P, K, R * E], F32, name="gate_%d" % h)
+            nc.scalar.activation(out=gate[h][:], in_=og_raw[h][:], func=ACT.Sigmoid)
 
-        def sigmoid_og(h, k0, k1):
-            t = sb.tile([P, k1 - k0, R * E], F32, name="gate_%d_%d" % (h, k0))
-            nc.scalar.activation(out=t[:], in_=og_raw[h][:, k0:k1, :], func=ACT.Sigmoid)
-            for k in range(k0, k1):
-                gate[h, k] = t[:, k - k0, :]
-
-        def copy_s(g):
+        def round_s(g):
             s_bf[g] = sb.tile([P, E, PACK], BF16, name="s_bf_%d" % g, align_bytes=64)
             nc.scalar.copy(
                 out=s_bf[g][:].rearrange("p (c i) j -> p c j i", i=4),
@@ -114,160 +89,127 @@ def tile_rows_read_sig_norm_gate_kernel(tc, q, qa, S, og, out):
                 in_=s_bf[g][:].rearrange("p e j -> p (e j)"),
             )
 
-        def new_xb(u):
-            xb[u] = sb.tile([P, R, P, PACK], BF16, name="xb_%d" % u, align_bytes=64)
-            codes[u] = sb.tile([P, R, P], U32, name="codes_%d" % u, align_bytes=64)
-            scales[u] = sb.tile([P, R, P], U8, name="scales_%d" % u, align_bytes=64)
-
-        def weigh_m(u, m0, m1):
-            if (u, "all") in sig:
-                src = sig[u, "all"][:, :, R * m0 : R * m1, :]
-            else:
-                src = sig[u, m0][:]
+        def weigh(u, half):
+            m0, m1 = HALVES[half]
+            if u not in q_bf:
+                q_bf[u] = sb.tile([P, R, P, PACK], BF16, name="q_bf_%d" % u, align_bytes=64)
+            qa_pairs = qa_t[:].rearrange("p (a b) -> p a b", b=2)
             nc.vector.tensor_tensor(
-                out=xb[u][:, :, m0:m1, :].rearrange("p r m (a b) -> p m r a b", b=2),
-                in0=src.rearrange("p a (m r) b -> p m r a b", r=R),
-                in1=qa_t[:].rearrange("p (a b) -> p a b", b=2).unsqueeze(1).unsqueeze(1).to_broadcast([P, m1 - m0, R, 2, 2]),
+                out=q_bf[u][:, :, m0:m1, :].rearrange("p r m (a b) -> p m r a b", b=2),
+                in0=phi[u][:, :, R * m0 : R * m1, :].rearrange("p a (m r) b -> p m r a b", r=R),
+                in1=qa_pairs.unsqueeze(1).unsqueeze(1).to_broadcast([P, m1 - m0, R, 2, 2]),
                 op=ALU.mult,
             )
 
-        def quant_q(u, r0, r1):
+        def quant_q(u):
+            q_codes[u] = sb.tile([P, R, P], U32, name="q_codes_%d" % u, align_bytes=64)
+            q_scales[u] = sb.tile([P, R, P], U8, name="q_scales_%d" % u, align_bytes=64)
             nc.vector.quantize_mx(
-                out=codes[u][:, r0:r1, :].rearrange("p r m -> p (r m)").bitcast(FP8X4),
-                scales=scales[u][:, r0:r1, :].rearrange("p r m -> p (r m)"),
-                in_=xb[u][:, r0:r1, :, :].rearrange("p r m j -> p (r m j)"),
+                out=q_codes[u][:].rearrange("p r m -> p (r m)").bitcast(FP8X4),
+                scales=q_scales[u][:].rearrange("p r m -> p (r m)"),
+                in_=q_bf[u][:].rearrange("p r m j -> p (r m j)"),
             )
 
-        def product(u, r):
-            g = UNITS[u][0]
-            for c in range(SIDE):
-                if (g, c) not in acc:
-                    acc[g, c] = ps.tile([P, 2 * R, E], F32, name="acc_%d_%d" % (g, c))
-                rows = slice(ROWS * c, ROWS * (c + 1))
-                nc.tensor.matmul_mx(
-                    out=acc[g, c][:, R * (u % 2) + r, :],
-                    lhsT=codes[u][rows, r, :].bitcast(FP8X4),
-                    lhsT_scale=scales[u][rows, r, :],
-                    rhs=s_codes[g][rows, :].bitcast(FP8X4),
-                    rhs_scale=s_scales[g][rows, :],
-                    start=True,
-                    stop=True,
-                )
+        def products(u):
+            g, k = divmod(u, K)
+            for r in range(R):
+                for c in range(SIDE):
+                    h = SIDE * g + c
+                    if h not in acc:
+                        acc[h] = ps.tile([P, K, R, E], F32, name="acc_%d" % h)
+                    rows = slice(ROWS * c, ROWS * (c + 1))
+                    nc.tensor.matmul_mx(
+                        out=acc[h][:, k, r, :],
+                        lhsT=q_codes[u][rows, r, :].bitcast(FP8X4),
+                        lhsT_scale=q_scales[u][rows, r, :],
+                        rhs=s_codes[g][rows, :].bitcast(FP8X4),
+                        rhs_scale=s_scales[g][rows, :],
+                        start=True,
+                        stop=True,
+                    )
 
         def inverse(h):
-            g, c = divmod(h, SIDE)
-            rec[g, c] = sb.tile([P, 2 * R], F32, name="rec_%d_%d" % (g, c))
-            nc.vector.reciprocal(out=rec[g, c][:], in_=acc[g, c][:, :, E - 1])
+            rec[h] = sb.tile([P, K, R], F32, name="rec_%d" % h)
+            nc.vector.reciprocal(out=rec[h][:], in_=acc[h][:, :, :, E - 1])
 
-        def finish(h, k, r0=0, r1=R):
-            g, c = divmod(h, SIDE)
-            t_out = sb.tile([P, (r1 - r0) * E], F32, name="res_%d_%d_%d" % (h, k, r0))
-            for r in range(r0, r1):
+        def store(h, k, result):
+            nc.sync.dma_start(out=head_rows(out, h)[:, k, :], in_=result[:])
+
+        def finish(h, k):
+            result = sb.tile([P, R * E], F32, name="result_%d_%d" % (h, k))
+            for r in range(R):
                 cols = slice(E * r, E * (r + 1))
-                t = R * k + r
                 nc.vector.scalar_tensor_tensor(
-                    out=t_out[:, E * (r - r0) : E * (r - r0 + 1)],
-                    in0=acc[g, c][:, t, :],
-                    scalar=rec[g, c][:, t : t + 1],
-                    in1=gate[h, k][:, cols],
+                    out=result[:, cols],
+                    in0=acc[h][:, k, r, :],
+                    scalar=rec[h][:, k, r : r + 1],
+                    in1=gate[h][:, k, cols],
                     op0=ALU.mult,
                     op1=ALU.mult,
                 )
-            nc.sync.dma_start(out=head_rows(out, h)[:, k, E * r0 : E * r1], in_=t_out[:])
+            store(h, k, result)
 
-        def normalise(h, k):
-            g, c = divmod(h, SIDE)
-            res[h, k] = sb.tile([P, R * E], F32, name="part_%d_%d" % (h, k))
+        def finish_off_vector(h, k):
+            divided = sb.tile([P, R * E], F32, name="divided")
+            result = sb.tile([P, R * E], F32, name="result_%d_%d" % (h, k))
             for r in range(R):
-                t = R * k + r
                 nc.scalar.activation(
-                    out=res[h, k][:, E * r : E * (r + 1)], in_=acc[g, c][:, t, :], func=ACT.Copy, scale=rec[g, c][:, t : t + 1]
+                    out=divided[:, E * r : E * (r + 1)],
+                    in_=acc[h][:, k, r, :],
+                    func=ACT.Copy,
+                    scale=rec[h][:, k, r : r + 1],
                 )
+            nc.gpsimd.tensor_tensor(out=result[:], in0=divided[:], in1=gate[h][:, k, :], op=ALU.mult)
+            return result
 
-        def gate_aside(h, k):
-            t_out = sb.tile([P, R * E], F32, name="res_%d_%d" % (h, k))
-            nc.gpsimd.tensor_tensor(out=t_out[:], in0=res[h, k][:], in1=gate[h, k], op=ALU.mult)
-            return t_out
-
-        def store_aside(h, k, t_out):
-            nc.sync.dma_start(out=head_rows(out, h)[:, k, :], in_=t_out[:])
-
-        def products(u):
-            for r in range(R):
-                product(u, r)
-
-        def sigmoid_unit(u, cuts, piece):
-            new_xb(u)
-            for m0, m1 in zip(cuts, cuts[1:]):
-                new_sig(u, m0, m1)
-                sigmoid_q(u, m0, m1, m0 - m0 % piece, m0)
-
-        HALF = P // 2
-        QUARTER = P // 4
-        def sigmoid_by_pairs(u):
-            sigmoid_pair(u, 0, 0, P)
-            sigmoid_pair(u, 1, 0, HALF)
-            sigmoid_pair(u, 1, HALF, P)
-
-        load_qa_pair(0, 0)
-        for c in range(SIDE):
-            nc.sync.dma_start(out=qa_t[ROWS * c : ROWS * (c + 1), :], in_=qa_rows)
-        load_qa_pair(0, 1)
-        load_qa_pair(1, 0)
-        load_qa_pair(1, 1)
-        load_qa_pair(2, 0)
-        load_qa_pair(2, 1)
+        load_q(0)
+        load_qa()
+        load_q(1)
+        load_q(2)
         load_s(0)
-        load_qa_pair(3, 0)
-        load_qa_pair(3, 1)
+        load_q(3)
         load_s(1)
-        load_og(0)
-        load_og(1)
-        load_og(2)
-        load_og(3)
+        for h in range(H):
+            load_og(h)
 
-        sigmoid_by_pairs(0)
-        sigmoid_by_pairs(1)
-        sigmoid_by_pairs(2)
-        copy_s(0)
-        sigmoid_by_pairs(3)
-        copy_s(1)
-        sigmoid_og(0, 0, 2)
-        sigmoid_og(1, 0, 2)
+        for u in range(3):
+            sigmoid_q(u)
+        round_s(0)
+        sigmoid_q(3)
+        round_s(1)
+        sigmoid_og(0)
+        sigmoid_og(1)
 
-        weigh_m(0, 0, HALF)
-        weigh_m(0, HALF, P)
-        quant_q(0, 0, R)
-        weigh_m(1, 0, HALF)
-        weigh_m(1, HALF, P)
-        weigh_m(2, 0, HALF)
-        quant_q(1, 0, R)
-        weigh_m(2, HALF, P)
+        weigh(0, 0)
+        weigh(0, 1)
+        quant_q(0)
+        weigh(1, 0)
+        weigh(1, 1)
+        weigh(2, 0)
+        quant_q(1)
+        weigh(2, 1)
         quant_s(0)
         products(0)
         products(1)
-        quant_q(2, 0, R)
-        weigh_m(3, 0, HALF)
-        weigh_m(3, HALF, P)
+        quant_q(2)
+        weigh(3, 0)
+        weigh(3, 1)
         quant_s(1)
         products(2)
         inverse(0)
         inverse(1)
-        quant_q(3, 0, 1)
-        product(3, 0)
-        quant_q(3, 1, 2)
-        product(3, 1)
-        normalise(1, 0)
-        aside_10 = gate_aside(1, 0)
-        sigmoid_og(2, 0, 2)
-        sigmoid_og(3, 0, 2)
+        quant_q(3)
+        products(3)
+
+        aside = finish_off_vector(1, 0)
+        sigmoid_og(2)
+        sigmoid_og(3)
         finish(0, 0)
         finish(0, 1)
         finish(1, 1)
         inverse(2)
         inverse(3)
-        store_aside(1, 0, aside_10)
-        finish(2, 0)
-        finish(2, 1)
-        finish(3, 0)
-        finish(3, 1)
+        store(1, 0, aside)
+        for h in (2, 3):
+            for k in range(K):
+                finish(h, k)

@@ -21,6 +21,7 @@ R = 2
 W = P * R
 K = N // W
 HALVES = ((0, P // 2), (P // 2, P))
+DMA_ALIGN = 256
 
 
 def tile_rows_read_sig_norm_gate_kernel(tc, q, qa, S, og, out):
@@ -45,7 +46,7 @@ def tile_rows_read_sig_norm_gate_kernel(tc, q, qa, S, og, out):
         def load_q(u):
             g, k = divmod(u, K)
             for a in range(2):
-                q_raw[u, a] = sb.tile([P, 2, W], F32, name="q_raw_%d_%d" % (u, a))
+                q_raw[u, a] = sb.tile([P, 2, W], F32, name="q_raw_%d_%d" % (u, a), align_bytes=DMA_ALIGN)
                 nc.sync.dma_start(out=q_raw[u, a][:], in_=q_rows[P * g : P * (g + 1), a, :, W * k : W * (k + 1)])
 
         def load_qa():
@@ -53,11 +54,11 @@ def tile_rows_read_sig_norm_gate_kernel(tc, q, qa, S, og, out):
                 nc.sync.dma_start(out=qa_t[ROWS * c : ROWS * (c + 1), :], in_=qa_rows)
 
         def load_s(g):
-            s_raw[g] = sb.tile([P, PACK, E], F32, name="s_raw_%d" % g)
+            s_raw[g] = sb.tile([P, PACK, E], F32, name="s_raw_%d" % g, align_bytes=DMA_ALIGN)
             nc.sync.dma_start(out=s_raw[g][:], in_=s_rows[P * g : P * (g + 1), :, :])
 
         def load_og(h):
-            og_raw[h] = sb.tile([P, K, R * E], F32, name="og_raw_%d" % h)
+            og_raw[h] = sb.tile([P, K, R * E], F32, name="og_raw_%d" % h, align_bytes=DMA_ALIGN)
             nc.sync.dma_start(out=og_raw[h][:], in_=head_rows(og, h))
 
         def sigmoid_q(u):
@@ -136,7 +137,7 @@ def tile_rows_read_sig_norm_gate_kernel(tc, q, qa, S, og, out):
             nc.sync.dma_start(out=head_rows(out, h)[:, k, :], in_=result[:])
 
         def finish(h, k):
-            result = sb.tile([P, R * E], F32, name="result_%d_%d" % (h, k))
+            result = sb.tile([P, R * E], F32, name="result_%d_%d" % (h, k), align_bytes=DMA_ALIGN)
             for r in range(R):
                 cols = slice(E * r, E * (r + 1))
                 nc.vector.scalar_tensor_tensor(
@@ -151,7 +152,7 @@ def tile_rows_read_sig_norm_gate_kernel(tc, q, qa, S, og, out):
 
         def finish_off_vector(h, k):
             divided = sb.tile([P, R * E], F32, name="divided")
-            result = sb.tile([P, R * E], F32, name="result_%d_%d" % (h, k))
+            result = sb.tile([P, R * E], F32, name="result_%d_%d" % (h, k), align_bytes=DMA_ALIGN)
             for r in range(R):
                 nc.scalar.activation(
                     out=divided[:, E * r : E * (r + 1)],

@@ -20,8 +20,9 @@ SIDE = P // ROWS
 R = 2
 W = P * R
 K = N // W
-HALVES = ((0, P // 2), (P // 2, P))
+STEPS = ((0, P // 4), (P // 4, P))
 DMA_ALIGN = 256
+WHOLE = (0, P)
 
 
 def tile_rows_read_sig_norm_gate_kernel(tc, q, qa, S, og, out):
@@ -61,9 +62,9 @@ def tile_rows_read_sig_norm_gate_kernel(tc, q, qa, S, og, out):
             og_raw[h] = sb.tile([P, K, R * E], F32, name="og_raw_%d" % h, align_bytes=DMA_ALIGN)
             nc.sync.dma_start(out=og_raw[h][:], in_=head_rows(og, h))
 
-        def sigmoid_q(u):
+        def sigmoid_q(u, steps):
             phi[u] = sb.tile([P, 2, W, 2], F32, name="phi_%d" % u)
-            for a, (m0, m1) in [(0, (0, P))] + [(1, half) for half in HALVES]:
+            for a, (m0, m1) in [(0, (0, P))] + [(1, step) for step in steps]:
                 nc.scalar.activation(
                     out=phi[u][:, a, R * m0 : R * m1, :],
                     in_=q_raw[u, a][:, :, R * m0 : R * m1].rearrange("p b n -> p n b"),
@@ -90,8 +91,8 @@ def tile_rows_read_sig_norm_gate_kernel(tc, q, qa, S, og, out):
                 in_=s_bf[g][:].rearrange("p e j -> p (e j)"),
             )
 
-        def weigh(u, half):
-            m0, m1 = HALVES[half]
+        def weigh(u, step):
+            m0, m1 = step
             if u not in q_bf:
                 q_bf[u] = sb.tile([P, R, P, PACK], BF16, name="q_bf_%d" % u, align_bytes=64)
             qa_pairs = qa_t[:].rearrange("p (a b) -> p a b", b=2)
@@ -173,32 +174,31 @@ def tile_rows_read_sig_norm_gate_kernel(tc, q, qa, S, og, out):
         for h in range(H):
             load_og(h)
 
-        for u in range(3):
-            sigmoid_q(u)
+        sigmoid_q(0, STEPS)
+        sigmoid_q(1, STEPS)
+        sigmoid_q(2, [WHOLE])
         round_s(0)
-        sigmoid_q(3)
+        sigmoid_q(3, [WHOLE])
         round_s(1)
         sigmoid_og(0)
         sigmoid_og(1)
 
-        weigh(0, 0)
-        weigh(0, 1)
+        weigh(0, STEPS[0])
+        weigh(0, STEPS[1])
+        weigh(1, STEPS[0])
         quant_q(0)
-        weigh(1, 0)
-        weigh(1, 1)
-        weigh(2, 0)
+        weigh(1, STEPS[1])
+        weigh(2, WHOLE)
         quant_q(1)
-        weigh(2, 1)
         quant_s(0)
         products(0)
         products(1)
         quant_q(2)
-        weigh(3, 0)
-        weigh(3, 1)
+        weigh(3, WHOLE)
+        inverse(1)
         quant_s(1)
         products(2)
         inverse(0)
-        inverse(1)
         quant_q(3)
         products(3)
 

@@ -22,6 +22,9 @@ W = P * R
 K = N // W
 STEPS = ((0, P // 4), (P // 4, P))
 DMA_ALIGN = 256
+SHARED = tuple(range(K))
+SPLIT_FROM = 4
+HALVES = ((0, P // 2), (P // 2, P))
 WHOLE = (0, P)
 
 
@@ -42,7 +45,7 @@ def tile_rows_read_sig_norm_gate_kernel(tc, q, qa, S, og, out):
         qa_t = sb.tile([P, PACK], F32, name="qa_t")
         q_raw, phi, q_bf, q_codes, q_scales = {}, {}, {}, {}, {}
         s_raw, s_bf, s_codes, s_scales = {}, {}, {}, {}
-        og_raw, gate, acc, rec = {}, {}, {}, {}
+        og_raw, gate, acc, rec, results = {}, {}, {}, {}, {}
 
         def load_q(u):
             g, k = divmod(u, K)
@@ -50,9 +53,27 @@ def tile_rows_read_sig_norm_gate_kernel(tc, q, qa, S, og, out):
                 q_raw[u, a] = sb.tile([P, 2, W], F32, name="q_raw_%d_%d" % (u, a), align_bytes=DMA_ALIGN)
                 nc.sync.dma_start(out=q_raw[u, a][:], in_=q_rows[P * g : P * (g + 1), a, :, W * k : W * (k + 1)])
 
-        def load_qa():
+        def load_q_rows(u, n0, n1):
+            g, k = divmod(u, K)
+            q_raw[u, n0, n1] = sb.tile([P, 2, 2, n1 - n0], F32, name="q_rows_%d_%d" % (u, n0), align_bytes=DMA_ALIGN)
+            nc.sync.dma_start(
+                out=q_raw[u, n0, n1][:].rearrange("p a b n -> p (a b) n"),
+                in_=q_rows[P * g : P * (g + 1), :, :, W * k + n0 : W * k + n1].rearrange("p a b n -> p (a b) n"),
+            )
+
+        def sigmoid_rows(u, n0, n1, step):
+            m0, m1 = step
+            if u not in phi:
+                phi[u] = sb.tile([P, 2, W, 2], F32, name="phi_%d" % u)
+            nc.scalar.activation(
+                out=phi[u][:, :, R * m0 : R * m1, :],
+                in_=q_raw[u, n0, n1][:, :, :, R * m0 - n0 : R * m1 - n0].rearrange("p a b n -> p a n b"),
+                func=ACT.Sigmoid,
+            )
+
+        def load_qa(queue):
             for c in range(SIDE):
-                nc.sync.dma_start(out=qa_t[ROWS * c : ROWS * (c + 1), :], in_=qa_rows)
+                queue.dma_start(out=qa_t[ROWS * c : ROWS * (c + 1), :], in_=qa_rows)
 
         def load_s(g):
             s_raw[g] = sb.tile([P, PACK, E], F32, name="s_raw_%d" % g, align_bytes=DMA_ALIGN)
@@ -112,16 +133,24 @@ def tile_rows_read_sig_norm_gate_kernel(tc, q, qa, S, og, out):
                 in_=q_bf[u][:].rearrange("p r m j -> p (r m j)"),
             )
 
+        def bank(h, k):
+            parts = SHARED if h < SPLIT_FROM else (k,)
+            if (h, parts) not in acc:
+                acc[h, parts] = ps.tile([P, len(parts), R, E], F32, name="acc_%d_%d" % (h, parts[0]))
+            return acc[h, parts], parts
+
+        def sums(h, k, r):
+            t, parts = bank(h, k)
+            return t[:, parts.index(k), r, :]
+
         def products(u):
             g, k = divmod(u, K)
             for r in range(R):
                 for c in range(SIDE):
                     h = SIDE * g + c
-                    if h not in acc:
-                        acc[h] = ps.tile([P, K, R, E], F32, name="acc_%d" % h)
                     rows = slice(ROWS * c, ROWS * (c + 1))
                     nc.tensor.matmul_mx(
-                        out=acc[h][:, k, r, :],
+                        out=sums(h, k, r),
                         lhsT=q_codes[u][rows, r, :].bitcast(FP8X4),
                         lhsT_scale=q_scales[u][rows, r, :],
                         rhs=s_codes[g][rows, :].bitcast(FP8X4),
@@ -130,87 +159,100 @@ def tile_rows_read_sig_norm_gate_kernel(tc, q, qa, S, og, out):
                         stop=True,
                     )
 
-        def inverse(h):
-            rec[h] = sb.tile([P, K, R], F32, name="rec_%d" % h)
-            nc.vector.reciprocal(out=rec[h][:], in_=acc[h][:, :, :, E - 1])
+        def inverse(h, k):
+            t, parts = bank(h, k)
+            inv = sb.tile([P, len(parts), R], F32, name="rec_%d_%d" % (h, k))
+            nc.vector.reciprocal(out=inv[:], in_=t[:, :, :, E - 1])
+            for i, part in enumerate(parts):
+                rec[h, part] = inv[:, i, :]
 
-        def store(h, k, result):
-            nc.sync.dma_start(out=head_rows(out, h)[:, k, :], in_=result[:])
+        def store(h, k, result, queue=nc.sync):
+            queue.dma_start(out=head_rows(out, h)[:, k, :], in_=result[:])
 
-        def finish(h, k):
-            result = sb.tile([P, R * E], F32, name="result_%d_%d" % (h, k), align_bytes=DMA_ALIGN)
-            for r in range(R):
+        def finish(h, k, tiles=tuple(range(R))):
+            if (h, k) not in results:
+                results[h, k] = sb.tile([P, R * E], F32, name="result_%d_%d" % (h, k), align_bytes=DMA_ALIGN)
+            result = results[h, k]
+            for r in tiles:
                 cols = slice(E * r, E * (r + 1))
                 nc.vector.scalar_tensor_tensor(
                     out=result[:, cols],
-                    in0=acc[h][:, k, r, :],
-                    scalar=rec[h][:, k, r : r + 1],
+                    in0=sums(h, k, r),
+                    scalar=rec[h, k][:, r : r + 1],
                     in1=gate[h][:, k, cols],
                     op0=ALU.mult,
                     op1=ALU.mult,
                 )
-            store(h, k, result)
+            return result
 
         def finish_off_vector(h, k):
-            divided = sb.tile([P, R * E], F32, name="divided")
+            divided = sb.tile([P, R * E], F32, name="divided_%d_%d" % (h, k))
             result = sb.tile([P, R * E], F32, name="result_%d_%d" % (h, k), align_bytes=DMA_ALIGN)
             for r in range(R):
                 nc.scalar.activation(
                     out=divided[:, E * r : E * (r + 1)],
-                    in_=acc[h][:, k, r, :],
+                    in_=sums(h, k, r),
                     func=ACT.Copy,
-                    scale=rec[h][:, k, r : r + 1],
+                    scale=rec[h, k][:, r : r + 1],
                 )
             nc.gpsimd.tensor_tensor(out=result[:], in0=divided[:], in1=gate[h][:, k, :], op=ALU.mult)
             return result
 
-        load_q(0)
-        load_qa()
-        load_q(1)
-        load_q(2)
+        load_qa(nc.scalar)
+        load_q_rows(0, 0, 128)
+        load_q_rows(0, 128, 256)
+
+        load_q_rows(1, 0, 128)
+        load_q_rows(1, 128, 256)
+        load_q_rows(2, 0, 128)
         load_s(0)
-        load_q(3)
+        load_q_rows(2, 128, 256)
+        load_q_rows(3, 0, 128)
+        load_q_rows(3, 128, 256)
         load_s(1)
         for h in range(H):
             load_og(h)
-
-        sigmoid_q(0, STEPS)
-        sigmoid_q(1, STEPS)
-        sigmoid_q(2, [WHOLE])
+        sigmoid_rows(0, 0, 128, HALVES[0])
+        sigmoid_rows(0, 128, 256, HALVES[1])
+        sigmoid_rows(1, 0, 128, HALVES[0])
+        sigmoid_rows(1, 128, 256, HALVES[1])
+        sigmoid_rows(2, 0, 128, HALVES[0])
         round_s(0)
-        sigmoid_q(3, [WHOLE])
+        sigmoid_rows(2, 128, 256, HALVES[1])
+        sigmoid_rows(3, 0, 128, HALVES[0])
+        sigmoid_rows(3, 128, 256, HALVES[1])
         round_s(1)
         sigmoid_og(0)
         sigmoid_og(1)
-
-        weigh(0, STEPS[0])
-        weigh(0, STEPS[1])
-        weigh(1, STEPS[0])
+        weigh(0, HALVES[0])
+        weigh(0, HALVES[1])
+        weigh(1, HALVES[0])
         quant_q(0)
-        weigh(1, STEPS[1])
-        weigh(2, WHOLE)
+        weigh(1, HALVES[1])
+        weigh(2, HALVES[0])
         quant_q(1)
         quant_s(0)
         products(0)
         products(1)
+        weigh(2, HALVES[1])
+        weigh(3, HALVES[0])
         quant_q(2)
-        weigh(3, WHOLE)
-        inverse(1)
+        weigh(3, HALVES[1])
         quant_s(1)
         products(2)
-        inverse(0)
+        inverse(1, 0)
+        inverse(0, 0)
         quant_q(3)
         products(3)
-
-        aside = finish_off_vector(1, 0)
+        a = finish_off_vector(1, 0)
         sigmoid_og(2)
         sigmoid_og(3)
-        finish(0, 0)
-        finish(0, 1)
-        finish(1, 1)
-        inverse(2)
-        inverse(3)
-        store(1, 0, aside)
+        store(0, 0, finish(0, 0))
+        store(0, 1, finish(0, 1))
+        store(1, 1, finish(1, 1))
+        inverse(2, 0)
+        inverse(3, 0)
+        store(1, 0, a)
         for h in (2, 3):
             for k in range(K):
-                finish(h, k)
+                store(h, k, finish(h, k))

@@ -25,6 +25,7 @@ DMA_ALIGN = 256
 SHARED = tuple(range(K))
 SPLIT_FROM = 4
 HALVES = ((0, P // 2), (P // 2, P))
+QUARTERS = tuple((P // 4 * i, P // 4 * (i + 1)) for i in range(4))
 WHOLE = (0, P)
 
 
@@ -143,10 +144,11 @@ def tile_rows_read_sig_norm_gate_kernel(tc, q, qa, S, og, out):
             t, parts = bank(h, k)
             return t[:, parts.index(k), r, :]
 
-        def products(u):
+        def products(u, by_heads=False):
             g, k = divmod(u, K)
-            for r in range(R):
-                for c in range(SIDE):
+            tiles = [(r, c) for r in range(R) for c in range(SIDE)]
+            for r, c in sorted(tiles, key=lambda t: t[1]) if by_heads else tiles:
+                if True:
                     h = SIDE * g + c
                     rows = slice(ROWS * c, ROWS * (c + 1))
                     nc.tensor.matmul_mx(
@@ -212,9 +214,12 @@ def tile_rows_read_sig_norm_gate_kernel(tc, q, qa, S, og, out):
         load_s(1)
         for h in range(H):
             load_og(h)
-        sigmoid_rows(0, 0, 128, HALVES[0])
-        sigmoid_rows(0, 128, 256, HALVES[1])
-        sigmoid_rows(1, 0, 128, HALVES[0])
+        sigmoid_rows(0, 0, 128, QUARTERS[0])
+        sigmoid_rows(0, 0, 128, QUARTERS[1])
+        sigmoid_rows(0, 128, 256, QUARTERS[2])
+        sigmoid_rows(0, 128, 256, QUARTERS[3])
+        sigmoid_rows(1, 0, 128, QUARTERS[0])
+        sigmoid_rows(1, 0, 128, QUARTERS[1])
         sigmoid_rows(1, 128, 256, HALVES[1])
         sigmoid_rows(2, 0, 128, HALVES[0])
         round_s(0)
@@ -224,9 +229,12 @@ def tile_rows_read_sig_norm_gate_kernel(tc, q, qa, S, og, out):
         round_s(1)
         sigmoid_og(0)
         sigmoid_og(1)
-        weigh(0, HALVES[0])
-        weigh(0, HALVES[1])
-        weigh(1, HALVES[0])
+        weigh(0, QUARTERS[0])
+        weigh(0, QUARTERS[1])
+        weigh(0, QUARTERS[2])
+        weigh(0, QUARTERS[3])
+        weigh(1, QUARTERS[0])
+        weigh(1, QUARTERS[1])
         quant_q(0)
         weigh(1, HALVES[1])
         weigh(2, HALVES[0])
@@ -243,14 +251,15 @@ def tile_rows_read_sig_norm_gate_kernel(tc, q, qa, S, og, out):
         inverse(1, 0)
         inverse(0, 0)
         quant_q(3)
-        products(3)
+        products(3, True)
         a = finish_off_vector(1, 0)
         sigmoid_og(2)
         sigmoid_og(3)
         store(0, 0, finish(0, 0))
         store(0, 1, finish(0, 1))
-        store(1, 1, finish(1, 1))
+        finish(1, 1, (0,))
         inverse(2, 0)
+        store(1, 1, finish(1, 1, (1,)))
         inverse(3, 0)
         store(1, 0, a)
         for h in (2, 3):

@@ -20,23 +20,26 @@ SIDE = P // ROWS
 R = 2
 W = P * R
 K = N // W
-STEPS = ((0, P // 4), (P // 4, P))
+LOADS = 2
+LOAD_M = P // LOADS
+STEPPED_LOADS = 3
 DMA_ALIGN = 256
-SHARED = tuple(range(K))
-SPLIT_FROM = 4
-HALVES = ((0, P // 2), (P // 2, P))
-QUARTERS = tuple((P // 4 * i, P // 4 * (i + 1)) for i in range(4))
-WHOLE = (0, P)
+
+
+def steps(u, i):
+    m0 = LOAD_M * i
+    if LOADS * u + i < STEPPED_LOADS:
+        return [(m0, m0 + LOAD_M // 2), (m0 + LOAD_M // 2, m0 + LOAD_M)]
+    return [(m0, m0 + LOAD_M)]
 
 
 def tile_rows_read_sig_norm_gate_kernel(tc, q, qa, S, og, out):
     nc = tc.nc
-    q_rows = q.rearrange("h (p a b) n -> (h p) a b n", a=2, b=2)
+    q_rows = q.rearrange("h (p j) n -> (h p) j n", j=PACK)
     s_rows = S.rearrange("h (p j) e -> (h p) j e", j=PACK)
     qa_rows = qa.rearrange("(p j) o -> p (j o)", j=PACK)
-
-    def head_rows(t, h):
-        return t[h].rearrange("(k m r) e -> m k (r e)", r=R, m=P)
+    og_halves = og.rearrange("h (k m r) e -> m h k (r e)", r=R, m=P)
+    out_halves = out.rearrange("h (k m r) e -> m h k (r e)", r=R, m=P)
 
     with ExitStack() as ctx:
         sb = ctx.enter_context(tc.tile_pool(name="sb", bufs=1))
@@ -46,56 +49,48 @@ def tile_rows_read_sig_norm_gate_kernel(tc, q, qa, S, og, out):
         qa_t = sb.tile([P, PACK], F32, name="qa_t")
         q_raw, phi, q_bf, q_codes, q_scales = {}, {}, {}, {}, {}
         s_raw, s_bf, s_codes, s_scales = {}, {}, {}, {}
-        og_raw, gate, acc, rec, results = {}, {}, {}, {}, {}
+        og_raw, gate, acc, rec, result = {}, {}, {}, {}, {}
 
-        def load_q(u):
-            g, k = divmod(u, K)
-            for a in range(2):
-                q_raw[u, a] = sb.tile([P, 2, W], F32, name="q_raw_%d_%d" % (u, a), align_bytes=DMA_ALIGN)
-                nc.sync.dma_start(out=q_raw[u, a][:], in_=q_rows[P * g : P * (g + 1), a, :, W * k : W * (k + 1)])
-
-        def load_q_rows(u, n0, n1):
-            g, k = divmod(u, K)
-            q_raw[u, n0, n1] = sb.tile([P, 2, 2, n1 - n0], F32, name="q_rows_%d_%d" % (u, n0), align_bytes=DMA_ALIGN)
-            nc.sync.dma_start(
-                out=q_raw[u, n0, n1][:].rearrange("p a b n -> p (a b) n"),
-                in_=q_rows[P * g : P * (g + 1), :, :, W * k + n0 : W * k + n1].rearrange("p a b n -> p (a b) n"),
-            )
-
-        def sigmoid_rows(u, n0, n1, step):
-            m0, m1 = step
-            if u not in phi:
-                phi[u] = sb.tile([P, 2, W, 2], F32, name="phi_%d" % u)
-            nc.scalar.activation(
-                out=phi[u][:, :, R * m0 : R * m1, :],
-                in_=q_raw[u, n0, n1][:, :, :, R * m0 - n0 : R * m1 - n0].rearrange("p a b n -> p a n b"),
-                func=ACT.Sigmoid,
-            )
-
-        def load_qa(queue):
+        def load_qa():
             for c in range(SIDE):
-                queue.dma_start(out=qa_t[ROWS * c : ROWS * (c + 1), :], in_=qa_rows)
+                nc.scalar.dma_start(out=qa_t[ROWS * c : ROWS * (c + 1), :], in_=qa_rows)
+
+        def load_q(u, i):
+            g, k = divmod(u, K)
+            n0 = W * k + R * LOAD_M * i
+            q_raw[u, i] = sb.tile([P, PACK, R * LOAD_M], F32, name="q_raw_%d_%d" % (u, i), align_bytes=DMA_ALIGN)
+            nc.sync.dma_start(out=q_raw[u, i][:], in_=q_rows[P * g : P * (g + 1), :, n0 : n0 + R * LOAD_M])
 
         def load_s(g):
             s_raw[g] = sb.tile([P, PACK, E], F32, name="s_raw_%d" % g, align_bytes=DMA_ALIGN)
             nc.sync.dma_start(out=s_raw[g][:], in_=s_rows[P * g : P * (g + 1), :, :])
 
-        def load_og(h):
-            og_raw[h] = sb.tile([P, K, R * E], F32, name="og_raw_%d" % h, align_bytes=DMA_ALIGN)
-            nc.sync.dma_start(out=og_raw[h][:], in_=head_rows(og, h))
+        def load_og_of_part(k):
+            both = sb.tile([P, SIDE, R * E], F32, name="og_part_%d" % k, align_bytes=DMA_ALIGN)
+            nc.sync.dma_start(out=both[:], in_=og_halves[:, 0:SIDE, k, :])
+            og_raw["part", k] = both
 
-        def sigmoid_q(u, steps):
-            phi[u] = sb.tile([P, 2, W, 2], F32, name="phi_%d" % u)
-            for a, (m0, m1) in [(0, (0, P))] + [(1, step) for step in steps]:
+        def load_og_of_head(h):
+            both = sb.tile([P, K, R * E], F32, name="og_head_%d" % h, align_bytes=DMA_ALIGN)
+            nc.sync.dma_start(out=both[:], in_=og_halves[:, h, :, :])
+            og_raw["head", h] = both
+
+        def sigmoid_q(u, i):
+            if u not in phi:
+                phi[u] = sb.tile([P, 2, W, 2], F32, name="phi_%d" % u)
+            first = R * LOAD_M * i
+            for m0, m1 in steps(u, i):
                 nc.scalar.activation(
-                    out=phi[u][:, a, R * m0 : R * m1, :],
-                    in_=q_raw[u, a][:, :, R * m0 : R * m1].rearrange("p b n -> p n b"),
+                    out=phi[u][:, :, R * m0 : R * m1, :],
+                    in_=q_raw[u, i][:, :, R * m0 - first : R * m1 - first].rearrange("p (a b) n -> p a n b", b=2),
                     func=ACT.Sigmoid,
                 )
 
-        def sigmoid_og(h):
-            gate[h] = sb.tile([P, K, R * E], F32, name="gate_%d" % h)
-            nc.scalar.activation(out=gate[h][:], in_=og_raw[h][:], func=ACT.Sigmoid)
+        def sigmoid_og(source, halves):
+            gates = sb.tile([P, len(halves), R * E], F32, name="gate_%d_%d" % halves[0])
+            nc.scalar.activation(out=gates[:], in_=source, func=ACT.Sigmoid)
+            for i, half in enumerate(halves):
+                gate[half] = gates[:, i, :]
 
         def round_s(g):
             s_bf[g] = sb.tile([P, E, PACK], BF16, name="s_bf_%d" % g, align_bytes=64)
@@ -113,17 +108,17 @@ def tile_rows_read_sig_norm_gate_kernel(tc, q, qa, S, og, out):
                 in_=s_bf[g][:].rearrange("p e j -> p (e j)"),
             )
 
-        def weigh(u, step):
-            m0, m1 = step
+        def weigh(u, i):
             if u not in q_bf:
                 q_bf[u] = sb.tile([P, R, P, PACK], BF16, name="q_bf_%d" % u, align_bytes=64)
             qa_pairs = qa_t[:].rearrange("p (a b) -> p a b", b=2)
-            nc.vector.tensor_tensor(
-                out=q_bf[u][:, :, m0:m1, :].rearrange("p r m (a b) -> p m r a b", b=2),
-                in0=phi[u][:, :, R * m0 : R * m1, :].rearrange("p a (m r) b -> p m r a b", r=R),
-                in1=qa_pairs.unsqueeze(1).unsqueeze(1).to_broadcast([P, m1 - m0, R, 2, 2]),
-                op=ALU.mult,
-            )
+            for m0, m1 in steps(u, i):
+                nc.vector.tensor_tensor(
+                    out=q_bf[u][:, :, m0:m1, :].rearrange("p r m (a b) -> p m r a b", b=2),
+                    in0=phi[u][:, :, R * m0 : R * m1, :].rearrange("p a (m r) b -> p m r a b", r=R),
+                    in1=qa_pairs.unsqueeze(1).unsqueeze(1).to_broadcast([P, m1 - m0, R, 2, 2]),
+                    op=ALU.mult,
+                )
 
         def quant_q(u):
             q_codes[u] = sb.tile([P, R, P], U32, name="q_codes_%d" % u, align_bytes=64)
@@ -134,134 +129,122 @@ def tile_rows_read_sig_norm_gate_kernel(tc, q, qa, S, og, out):
                 in_=q_bf[u][:].rearrange("p r m j -> p (r m j)"),
             )
 
-        def bank(h, k):
-            parts = SHARED if h < SPLIT_FROM else (k,)
-            if (h, parts) not in acc:
-                acc[h, parts] = ps.tile([P, len(parts), R, E], F32, name="acc_%d_%d" % (h, parts[0]))
-            return acc[h, parts], parts
-
-        def sums(h, k, r):
-            t, parts = bank(h, k)
-            return t[:, parts.index(k), r, :]
-
-        def products(u, by_heads=False):
+        def products(u):
             g, k = divmod(u, K)
-            tiles = [(r, c) for r in range(R) for c in range(SIDE)]
-            for r, c in sorted(tiles, key=lambda t: t[1]) if by_heads else tiles:
-                if True:
-                    h = SIDE * g + c
-                    rows = slice(ROWS * c, ROWS * (c + 1))
-                    nc.tensor.matmul_mx(
-                        out=sums(h, k, r),
-                        lhsT=q_codes[u][rows, r, :].bitcast(FP8X4),
-                        lhsT_scale=q_scales[u][rows, r, :],
-                        rhs=s_codes[g][rows, :].bitcast(FP8X4),
-                        rhs_scale=s_scales[g][rows, :],
-                        start=True,
-                        stop=True,
-                    )
-
-        def inverse(h, k):
-            t, parts = bank(h, k)
-            inv = sb.tile([P, len(parts), R], F32, name="rec_%d_%d" % (h, k))
-            nc.vector.reciprocal(out=inv[:], in_=t[:, :, :, E - 1])
-            for i, part in enumerate(parts):
-                rec[h, part] = inv[:, i, :]
-
-        def store(h, k, result, queue=nc.sync):
-            queue.dma_start(out=head_rows(out, h)[:, k, :], in_=result[:])
-
-        def finish(h, k, tiles=tuple(range(R))):
-            if (h, k) not in results:
-                results[h, k] = sb.tile([P, R * E], F32, name="result_%d_%d" % (h, k), align_bytes=DMA_ALIGN)
-            result = results[h, k]
-            for r in tiles:
-                cols = slice(E * r, E * (r + 1))
-                nc.vector.scalar_tensor_tensor(
-                    out=result[:, cols],
-                    in0=sums(h, k, r),
-                    scalar=rec[h, k][:, r : r + 1],
-                    in1=gate[h][:, k, cols],
-                    op0=ALU.mult,
-                    op1=ALU.mult,
+            if k < K - 1:
+                tiles = [(c, r) for r in range(R) for c in range(SIDE)]
+            else:
+                tiles = [(h - SIDE * g, r) for h in inverted_in_order[g] for r in range(R)]
+            for c, r in tiles:
+                h = SIDE * g + c
+                if h not in acc:
+                    acc[h] = ps.tile([P, K, R, E], F32, name="acc_%d" % h)
+                rows = slice(ROWS * c, ROWS * (c + 1))
+                nc.tensor.matmul_mx(
+                    out=acc[h][:, k, r, :],
+                    lhsT=q_codes[u][rows, r, :].bitcast(FP8X4),
+                    lhsT_scale=q_scales[u][rows, r, :],
+                    rhs=s_codes[g][rows, :].bitcast(FP8X4),
+                    rhs_scale=s_scales[g][rows, :],
+                    start=True,
+                    stop=True,
                 )
-            return result
+
+        def inverse(h):
+            rec[h] = sb.tile([P, K, R], F32, name="rec_%d" % h)
+            nc.vector.reciprocal(out=rec[h][:], in_=acc[h][:, :, :, E - 1])
+
+        def result_tile(h, k):
+            if (h, k) not in result:
+                result[h, k] = sb.tile([P, R * E], F32, name="result_%d_%d" % (h, k), align_bytes=DMA_ALIGN)
+            return result[h, k]
+
+        def store(h, k):
+            nc.sync.dma_start(out=out_halves[:, h, k, :], in_=result[h, k][:])
+
+        def finish_tile(h, k, r):
+            cols = slice(E * r, E * (r + 1))
+            nc.vector.scalar_tensor_tensor(
+                out=result_tile(h, k)[:, cols],
+                in0=acc[h][:, k, r, :],
+                scalar=rec[h][:, k, r : r + 1],
+                in1=gate[h, k][:, cols],
+                op0=ALU.mult,
+                op1=ALU.mult,
+            )
+
+        def finish(h, k):
+            for r in range(R):
+                finish_tile(h, k, r)
+            store(h, k)
 
         def finish_off_vector(h, k):
-            divided = sb.tile([P, R * E], F32, name="divided_%d_%d" % (h, k))
-            result = sb.tile([P, R * E], F32, name="result_%d_%d" % (h, k), align_bytes=DMA_ALIGN)
+            divided = sb.tile([P, R * E], F32, name="divided")
             for r in range(R):
                 nc.scalar.activation(
                     out=divided[:, E * r : E * (r + 1)],
-                    in_=sums(h, k, r),
+                    in_=acc[h][:, k, r, :],
                     func=ACT.Copy,
-                    scale=rec[h, k][:, r : r + 1],
+                    scale=rec[h][:, k, r : r + 1],
                 )
-            nc.gpsimd.tensor_tensor(out=result[:], in0=divided[:], in1=gate[h][:, k, :], op=ALU.mult)
-            return result
+            nc.gpsimd.tensor_tensor(out=result_tile(h, k)[:], in0=divided[:], in1=gate[h, k], op=ALU.mult)
 
-        load_qa(nc.scalar)
-        load_q_rows(0, 0, 128)
-        load_q_rows(0, 128, 256)
+        inverted_in_order = {0: (1, 0), 1: (2, 3)}
 
-        load_q_rows(1, 0, 128)
-        load_q_rows(1, 128, 256)
-        load_q_rows(2, 0, 128)
+        load_qa()
+        for u, i in ((0, 0), (0, 1), (1, 0), (1, 1), (2, 0)):
+            load_q(u, i)
         load_s(0)
-        load_q_rows(2, 128, 256)
-        load_q_rows(3, 0, 128)
-        load_q_rows(3, 128, 256)
+        for u, i in ((2, 1), (3, 0), (3, 1)):
+            load_q(u, i)
         load_s(1)
-        for h in range(H):
-            load_og(h)
-        sigmoid_rows(0, 0, 128, QUARTERS[0])
-        sigmoid_rows(0, 0, 128, QUARTERS[1])
-        sigmoid_rows(0, 128, 256, QUARTERS[2])
-        sigmoid_rows(0, 128, 256, QUARTERS[3])
-        sigmoid_rows(1, 0, 128, QUARTERS[0])
-        sigmoid_rows(1, 0, 128, QUARTERS[1])
-        sigmoid_rows(1, 128, 256, HALVES[1])
-        sigmoid_rows(2, 0, 128, HALVES[0])
+        for k in range(K):
+            load_og_of_part(k)
+        for h in (2, 3):
+            load_og_of_head(h)
+
+        for u, i in ((0, 0), (0, 1), (1, 0), (1, 1), (2, 0)):
+            sigmoid_q(u, i)
         round_s(0)
-        sigmoid_rows(2, 128, 256, HALVES[1])
-        sigmoid_rows(3, 0, 128, HALVES[0])
-        sigmoid_rows(3, 128, 256, HALVES[1])
+        for u, i in ((2, 1), (3, 0), (3, 1)):
+            sigmoid_q(u, i)
         round_s(1)
-        sigmoid_og(0)
-        sigmoid_og(1)
-        weigh(0, QUARTERS[0])
-        weigh(0, QUARTERS[1])
-        weigh(0, QUARTERS[2])
-        weigh(0, QUARTERS[3])
-        weigh(1, QUARTERS[0])
-        weigh(1, QUARTERS[1])
+        sigmoid_og(og_raw["part", 0][:], [(0, 0), (1, 0)])
+
+        weigh(0, 0)
+        weigh(0, 1)
+        weigh(1, 0)
         quant_q(0)
-        weigh(1, HALVES[1])
-        weigh(2, HALVES[0])
-        quant_q(1)
+        weigh(1, 1)
+        weigh(2, 0)
         quant_s(0)
         products(0)
+        quant_q(1)
         products(1)
-        weigh(2, HALVES[1])
-        weigh(3, HALVES[0])
+        weigh(2, 1)
+        weigh(3, 0)
         quant_q(2)
-        weigh(3, HALVES[1])
+        inverse(1)
+        weigh(3, 1)
         quant_s(1)
         products(2)
-        inverse(1, 0)
-        inverse(0, 0)
+        inverse(0)
         quant_q(3)
-        products(3, True)
-        a = finish_off_vector(1, 0)
-        sigmoid_og(2)
-        sigmoid_og(3)
-        store(0, 0, finish(0, 0))
-        store(0, 1, finish(0, 1))
-        finish(1, 1, (0,))
-        inverse(2, 0)
-        store(1, 1, finish(1, 1, (1,)))
-        inverse(3, 0)
-        store(1, 0, a)
+        products(3)
+
+        finish_off_vector(1, 0)
+        for h in range(SIDE):
+            sigmoid_og(og_raw["part", 1][:, h : h + 1, :], [(h, 1)])
+        for h in (2, 3):
+            sigmoid_og(og_raw["head", h][:], [(h, 0), (h, 1)])
+        finish(0, 0)
+        finish(0, 1)
+        store(1, 0)
+        finish_tile(1, 1, 0)
+        inverse(2)
+        finish_tile(1, 1, 1)
+        store(1, 1)
+        inverse(3)
         for h in (2, 3):
             for k in range(K):
-                store(h, k, finish(h, k))
+                finish(h, k)

@@ -20,17 +20,7 @@ SIDE = P // ROWS
 R = 2
 W = P * R
 K = N // W
-LOADS = 2
-LOAD_M = P // LOADS
-STEPPED_LOADS = 3
 DMA_ALIGN = 256
-
-
-def steps(u, i):
-    m0 = LOAD_M * i
-    if LOADS * u + i < STEPPED_LOADS:
-        return [(m0, m0 + LOAD_M // 2), (m0 + LOAD_M // 2, m0 + LOAD_M)]
-    return [(m0, m0 + LOAD_M)]
 
 
 def tile_rows_read_sig_norm_gate_kernel(tc, q, qa, S, og, out):
@@ -49,54 +39,72 @@ def tile_rows_read_sig_norm_gate_kernel(tc, q, qa, S, og, out):
         qa_t = sb.tile([P, PACK], F32, name="qa_t")
         q_raw, phi, q_bf, q_codes, q_scales = {}, {}, {}, {}, {}
         s_raw, s_bf, s_codes, s_scales = {}, {}, {}, {}
-        og_raw, gate, acc, rec, result = {}, {}, {}, {}, {}
+        og_raw, gate, acc, rec, result, divided = {}, {}, {}, {}, {}, {}
 
         def load_qa():
-            for c in range(SIDE):
-                nc.scalar.dma_start(out=qa_t[ROWS * c : ROWS * (c + 1), :], in_=qa_rows)
+            nc.scalar.dma_start(out=qa_t[:], in_=qa_rows.partition_broadcast(SIDE))
 
-        def load_q(u, i):
+        def load_q(u, m0, m1):
             g, k = divmod(u, K)
-            n0 = W * k + R * LOAD_M * i
-            q_raw[u, i] = sb.tile([P, PACK, R * LOAD_M], F32, name="q_raw_%d_%d" % (u, i), align_bytes=DMA_ALIGN)
-            nc.sync.dma_start(out=q_raw[u, i][:], in_=q_rows[P * g : P * (g + 1), :, n0 : n0 + R * LOAD_M])
+            raw = sb.tile([P, PACK, R * (m1 - m0)], F32, name="q_raw_%d_%d" % (u, m0), align_bytes=DMA_ALIGN)
+            nc.sync.dma_start(out=raw[:], in_=q_rows[P * g : P * (g + 1), :, W * k + R * m0 : W * k + R * m1])
+            q_raw[u, m0] = raw
 
         def load_s(g):
             s_raw[g] = sb.tile([P, PACK, E], F32, name="s_raw_%d" % g, align_bytes=DMA_ALIGN)
             nc.sync.dma_start(out=s_raw[g][:], in_=s_rows[P * g : P * (g + 1), :, :])
 
-        def load_og_of_part(k):
-            both = sb.tile([P, SIDE, R * E], F32, name="og_part_%d" % k, align_bytes=DMA_ALIGN)
-            nc.sync.dma_start(out=both[:], in_=og_halves[:, 0:SIDE, k, :])
-            og_raw["part", k] = both
+        def load_og(heads, parts):
+            raw = sb.tile(
+                [P, len(heads), len(parts), R * E], F32, name="og_%d_%d" % (heads[0], parts[0]), align_bytes=DMA_ALIGN
+            )
+            nc.sync.dma_start(out=raw[:], in_=og_halves[:, heads[0] : heads[-1] + 1, parts[0] : parts[-1] + 1, :])
+            for i, h in enumerate(heads):
+                for n, k in enumerate(parts):
+                    og_raw[h, k] = (raw, i, n)
 
-        def load_og_of_head(h):
-            both = sb.tile([P, K, R * E], F32, name="og_head_%d" % h, align_bytes=DMA_ALIGN)
-            nc.sync.dma_start(out=both[:], in_=og_halves[:, h, :, :])
-            og_raw["head", h] = both
-
-        def sigmoid_q(u, i):
+        def sigmoid_q(u, m0, m1):
             if u not in phi:
                 phi[u] = sb.tile([P, 2, W, 2], F32, name="phi_%d" % u)
-            first = R * LOAD_M * i
-            for m0, m1 in steps(u, i):
-                nc.scalar.activation(
-                    out=phi[u][:, :, R * m0 : R * m1, :],
-                    in_=q_raw[u, i][:, :, R * m0 - first : R * m1 - first].rearrange("p (a b) n -> p a n b", b=2),
-                    func=ACT.Sigmoid,
-                )
+            first = max(m for v, m in q_raw if v == u and m <= m0)
+            nc.scalar.activation(
+                out=phi[u][:, :, R * m0 : R * m1, :],
+                in_=q_raw[u, first][:, :, R * (m0 - first) : R * (m1 - first)].rearrange("p (a b) n -> p a n b", b=2),
+                func=ACT.Sigmoid,
+            )
 
-        def sigmoid_og(source, halves):
-            gates = sb.tile([P, len(halves), R * E], F32, name="gate_%d_%d" % halves[0])
-            nc.scalar.activation(out=gates[:], in_=source, func=ACT.Sigmoid)
-            for i, half in enumerate(halves):
-                gate[half] = gates[:, i, :]
+        def sigmoid_og(heads, parts):
+            raw, i0, n0 = og_raw[heads[0], parts[0]]
+            gates = sb.tile([P, len(heads), len(parts), R * E], F32, name="gate_%d_%d" % (heads[0], parts[0]))
+            nc.scalar.activation(out=gates[:], in_=raw[:, i0 : i0 + len(heads), n0 : n0 + len(parts), :], func=ACT.Sigmoid)
+            for i, h in enumerate(heads):
+                for n, k in enumerate(parts):
+                    gate[h, k] = gates[:, i, n, :]
 
-        def round_s(g):
+        def s_views(g):
             s_bf[g] = sb.tile([P, E, PACK], BF16, name="s_bf_%d" % g, align_bytes=64)
-            nc.scalar.copy(
-                out=s_bf[g][:].rearrange("p (c i) j -> p c j i", i=4),
-                in_=s_raw[g][:].rearrange("p j (c i) -> p c j i", i=4),
+            return (
+                s_bf[g][:].rearrange("p (c i) j -> p c j i", i=4),
+                s_raw[g][:].rearrange("p j (c i) -> p c j i", i=4),
+            )
+
+        def round_s_on_scalar(g):
+            dst, src = s_views(g)
+            nc.scalar.copy(out=dst, in_=src)
+
+        def round_s_on_vector(g):
+            dst, src = s_views(g)
+            nc.vector.tensor_copy(out=dst, in_=src)
+
+        def round_s_on_gpsimd(g):
+            s_bf[g] = sb.tile([P, E, PACK], BF16, name="s_bf_%d" % g, align_bytes=64)
+            nc.gpsimd.tensor_scalar(
+                out=s_bf[g][:],
+                in0=s_raw[g][:].rearrange("p j e -> p e j"),
+                scalar1=1.0,
+                scalar2=0.0,
+                op0=ALU.mult,
+                op1=ALU.add,
             )
 
         def quant_s(g):
@@ -108,17 +116,16 @@ def tile_rows_read_sig_norm_gate_kernel(tc, q, qa, S, og, out):
                 in_=s_bf[g][:].rearrange("p e j -> p (e j)"),
             )
 
-        def weigh(u, i):
+        def weigh(u, m0, m1):
             if u not in q_bf:
-                q_bf[u] = sb.tile([P, R, P, PACK], BF16, name="q_bf_%d" % u, align_bytes=64)
+                q_bf[u] = sb.tile([P, R, P, PACK], BF16, name="q_bf_%d" % u, align_bytes=DMA_ALIGN)
             qa_pairs = qa_t[:].rearrange("p (a b) -> p a b", b=2)
-            for m0, m1 in steps(u, i):
-                nc.vector.tensor_tensor(
-                    out=q_bf[u][:, :, m0:m1, :].rearrange("p r m (a b) -> p m r a b", b=2),
-                    in0=phi[u][:, :, R * m0 : R * m1, :].rearrange("p a (m r) b -> p m r a b", r=R),
-                    in1=qa_pairs.unsqueeze(1).unsqueeze(1).to_broadcast([P, m1 - m0, R, 2, 2]),
-                    op=ALU.mult,
-                )
+            nc.vector.tensor_tensor(
+                out=q_bf[u][:, :, m0:m1, :].rearrange("p r m (a b) -> p m r a b", b=2),
+                in0=phi[u][:, :, R * m0 : R * m1, :].rearrange("p a (m r) b -> p m r a b", r=R),
+                in1=qa_pairs.unsqueeze(1).unsqueeze(1).to_broadcast([P, m1 - m0, R, 2, 2]),
+                op=ALU.mult,
+            )
 
         def quant_q(u):
             q_codes[u] = sb.tile([P, R, P], U32, name="q_codes_%d" % u, align_bytes=64)
@@ -129,19 +136,18 @@ def tile_rows_read_sig_norm_gate_kernel(tc, q, qa, S, og, out):
                 in_=q_bf[u][:].rearrange("p r m j -> p (r m j)"),
             )
 
-        def products(u):
+        def bank(name, halves):
+            sums = ps.tile([P, len(halves), R, E], F32, name=name)
+            for i, half in enumerate(halves):
+                acc[half] = (sums, i)
+
+        def products(u, tiles):
             g, k = divmod(u, K)
-            if k < K - 1:
-                tiles = [(c, r) for r in range(R) for c in range(SIDE)]
-            else:
-                tiles = [(h - SIDE * g, r) for h in inverted_in_order[g] for r in range(R)]
             for c, r in tiles:
-                h = SIDE * g + c
-                if h not in acc:
-                    acc[h] = ps.tile([P, K, R, E], F32, name="acc_%d" % h)
+                sums, i = acc[SIDE * g + c, k]
                 rows = slice(ROWS * c, ROWS * (c + 1))
                 nc.tensor.matmul_mx(
-                    out=acc[h][:, k, r, :],
+                    out=sums[:, i, r, :],
                     lhsT=q_codes[u][rows, r, :].bitcast(FP8X4),
                     lhsT_scale=q_scales[u][rows, r, :],
                     rhs=s_codes[g][rows, :].bitcast(FP8X4),
@@ -150,24 +156,40 @@ def tile_rows_read_sig_norm_gate_kernel(tc, q, qa, S, og, out):
                     stop=True,
                 )
 
-        def inverse(h):
-            rec[h] = sb.tile([P, K, R], F32, name="rec_%d" % h)
-            nc.vector.reciprocal(out=rec[h][:], in_=acc[h][:, :, :, E - 1])
+        def inverse(halves):
+            sums, i0 = acc[halves[0]]
+            inv = sb.tile([P, len(halves), R], F32, name="rec_%d_%d" % halves[0])
+            nc.vector.reciprocal(out=inv[:], in_=sums[:, i0 : i0 + len(halves), :, E - 1])
+            for i, half in enumerate(halves):
+                rec[half] = inv[:, i, :]
 
-        def result_tile(h, k):
+        def results(heads, parts, tag=None):
+            name = "result_%d_%d" % (heads[0], parts[0])
+            both = sb.tile([P, len(heads), len(parts), R * E], F32, name=name, tag=tag or name, align_bytes=DMA_ALIGN)
+            for i, h in enumerate(heads):
+                for n, k in enumerate(parts):
+                    result[h, k] = (both, i, n)
+
+        def result_of(h, k):
             if (h, k) not in result:
-                result[h, k] = sb.tile([P, R * E], F32, name="result_%d_%d" % (h, k), align_bytes=DMA_ALIGN)
-            return result[h, k]
+                results([h], [k])
+            both, i, n = result[h, k]
+            return both[:, i, n, :]
 
-        def store(h, k):
-            nc.sync.dma_start(out=out_halves[:, h, k, :], in_=result[h, k][:])
+        def store(heads, parts):
+            both, i0, n0 = result[heads[0], parts[0]]
+            nc.sync.dma_start(
+                out=out_halves[:, heads[0] : heads[-1] + 1, parts[0] : parts[-1] + 1, :],
+                in_=both[:, i0 : i0 + len(heads), n0 : n0 + len(parts), :],
+            )
 
         def finish_tile(h, k, r):
             cols = slice(E * r, E * (r + 1))
+            sums, i = acc[h, k]
             nc.vector.scalar_tensor_tensor(
-                out=result_tile(h, k)[:, cols],
-                in0=acc[h][:, k, r, :],
-                scalar=rec[h][:, k, r : r + 1],
+                out=result_of(h, k)[:, cols],
+                in0=sums[:, i, r, :],
+                scalar=rec[h, k][:, r : r + 1],
                 in1=gate[h, k][:, cols],
                 op0=ALU.mult,
                 op1=ALU.mult,
@@ -176,75 +198,93 @@ def tile_rows_read_sig_norm_gate_kernel(tc, q, qa, S, og, out):
         def finish(h, k):
             for r in range(R):
                 finish_tile(h, k, r)
-            store(h, k)
 
-        def finish_off_vector(h, k):
-            divided = sb.tile([P, R * E], F32, name="divided")
+        def divide(h, k):
+            sums, i = acc[h, k]
+            divided[h, k] = sb.tile([P, R * E], F32, name="divided_%d_%d" % (h, k))
             for r in range(R):
                 nc.scalar.activation(
-                    out=divided[:, E * r : E * (r + 1)],
-                    in_=acc[h][:, k, r, :],
+                    out=divided[h, k][:, E * r : E * (r + 1)],
+                    in_=sums[:, i, r, :],
                     func=ACT.Copy,
-                    scale=rec[h][:, k, r : r + 1],
+                    scale=rec[h, k][:, r : r + 1],
                 )
-            nc.gpsimd.tensor_tensor(out=result_tile(h, k)[:], in0=divided[:], in1=gate[h, k], op=ALU.mult)
 
-        inverted_in_order = {0: (1, 0), 1: (2, 3)}
+        def apply_gate(h, k):
+            nc.gpsimd.tensor_tensor(out=result_of(h, k), in0=divided[h, k][:], in1=gate[h, k], op=ALU.mult)
 
-        load_qa()
-        for u, i in ((0, 0), (0, 1), (1, 0), (1, 1), (2, 0)):
-            load_q(u, i)
-        load_s(0)
-        for u, i in ((2, 1), (3, 0), (3, 1)):
-            load_q(u, i)
-        load_s(1)
+        in_turn = [(c, r) for r in range(R) for c in range(SIDE)]
+
+        for h in (0, 2, 3):
+            bank("acc_%d" % h, [(h, 0), (h, 1)])
         for k in range(K):
-            load_og_of_part(k)
-        for h in (2, 3):
-            load_og_of_head(h)
+            bank("acc_1_%d" % k, [(1, k)])
+        load_qa()
+        for u in (0, 1, 2):
+            load_q(u, 0, 64)
+            load_q(u, 64, 128)
+        load_s(0)
+        load_q(3, 0, 64)
+        load_q(3, 64, 128)
+        load_s(1)
+        load_og([0, 1], [0])
+        load_og([0, 1], [1])
+        load_og([2], [0, 1])
+        load_og([3], [0])
+        load_og([3], [1])
 
-        for u, i in ((0, 0), (0, 1), (1, 0), (1, 1), (2, 0)):
-            sigmoid_q(u, i)
-        round_s(0)
-        for u, i in ((2, 1), (3, 0), (3, 1)):
-            sigmoid_q(u, i)
-        round_s(1)
-        sigmoid_og(og_raw["part", 0][:], [(0, 0), (1, 0)])
+        for m0 in range(0, 128, 32):
+            sigmoid_q(0, m0, m0 + 32)
+        sigmoid_q(1, 0, 32)
+        sigmoid_q(1, 32, 64)
+        sigmoid_q(1, 64, 128)
+        sigmoid_q(2, 0, 64)
+        sigmoid_q(2, 64, 128)
+        round_s_on_scalar(0)
+        sigmoid_q(3, 0, 64)
+        sigmoid_q(3, 64, 128)
+        round_s_on_scalar(1)
+        sigmoid_og([0, 1], [0])
 
-        weigh(0, 0)
-        weigh(0, 1)
-        weigh(1, 0)
+        for m0 in range(0, 128, 32):
+            weigh(0, m0, m0 + 32)
+        weigh(1, 0, 32)
+        weigh(1, 32, 64)
         quant_q(0)
-        weigh(1, 1)
-        weigh(2, 0)
-        quant_s(0)
-        products(0)
+        weigh(1, 64, 128)
+        weigh(2, 0, 64)
+        weigh(2, 64, 128)
         quant_q(1)
-        products(1)
-        weigh(2, 1)
-        weigh(3, 0)
+        quant_s(0)
+        products(0, in_turn)
+        products(1, in_turn)
         quant_q(2)
-        inverse(1)
-        weigh(3, 1)
+        weigh(3, 0, 64)
+        weigh(3, 64, 128)
         quant_s(1)
-        products(2)
-        inverse(0)
+        products(2, in_turn)
+        inverse([(1, 0)])
+        inverse([(0, 0), (0, 1)])
         quant_q(3)
-        products(3)
-
-        finish_off_vector(1, 0)
-        for h in range(SIDE):
-            sigmoid_og(og_raw["part", 1][:, h : h + 1, :], [(h, 1)])
+        inverse([(1, 1)])
+        products(3, [(0, 0), (0, 1), (1, 0), (1, 1)])
+        sigmoid_og([0], [1])
+        sigmoid_og([1], [1])
+        divide(1, 0)
+        apply_gate(1, 0)
         for h in (2, 3):
-            sigmoid_og(og_raw["head", h][:], [(h, 0), (h, 1)])
+            for k in range(K):
+                sigmoid_og([h], [k])
         finish(0, 0)
+        store([0], [0])
         finish(0, 1)
-        store(1, 0)
-        finish_tile(1, 1, 0)
-        inverse(2)
-        finish_tile(1, 1, 1)
-        store(1, 1)
-        inverse(3)
+        store([0], [1])
+        finish(1, 1)
+        store([1], [1])
+        inverse([(2, 0), (2, 1)])
+        inverse([(3, 0), (3, 1)])
+        store([1], [0])
         for h in (2, 3):
             for k in range(K):
                 finish(h, k)
+                store([h], [k])

@@ -42,7 +42,8 @@ def tile_rows_read_sig_norm_gate_kernel(tc, q, qa, S, og, out):
         og_raw, gate, acc, rec, result, divided = {}, {}, {}, {}, {}, {}
 
         def load_qa():
-            nc.scalar.dma_start(out=qa_t[:], in_=qa_rows.partition_broadcast(SIDE))
+            for c in range(SIDE):
+                nc.scalar.dma_start(out=qa_t[ROWS * c : ROWS * (c + 1), :], in_=qa_rows)
 
         def load_q(u, m0, m1):
             g, k = divmod(u, K)
@@ -230,8 +231,7 @@ def tile_rows_read_sig_norm_gate_kernel(tc, q, qa, S, og, out):
         load_og([0, 1], [0])
         load_og([0, 1], [1])
         load_og([2], [0, 1])
-        load_og([3], [0])
-        load_og([3], [1])
+        load_og([3], [0, 1])
 
         for m0 in range(0, 128, 32):
             sigmoid_q(0, m0, m0 + 32)
@@ -283,8 +283,11 @@ def tile_rows_read_sig_norm_gate_kernel(tc, q, qa, S, og, out):
         store([1], [1])
         inverse([(2, 0), (2, 1)])
         inverse([(3, 0), (3, 1)])
+        finish(2, 0)
+        store([2], [0])
         store([1], [0])
-        for h in (2, 3):
-            for k in range(K):
-                finish(h, k)
-                store([h], [k])
+        finish(2, 1)
+        store([2], [1])
+        for k in range(K):
+            finish(3, k)
+            store([3], [k])

@@ -26,7 +26,7 @@ DMA_ALIGN = 256
 def tile_rows_read_sig_norm_gate_kernel(tc, q, qa, S, og, out):
     nc = tc.nc
     q_rows = q.rearrange("h (p j) n -> (h p) j n", j=PACK)
-    s_rows = S.rearrange("h (p j) e -> (h p) j e", j=PACK)
+    s_rows = S.rearrange("(g c) (p j) e -> (c p) g (j e)", c=SIDE, j=PACK)
     qa_rows = qa.rearrange("(p j) o -> p (j o)", j=PACK)
     og_halves = og.rearrange("h (k m r) e -> m h k (r e)", r=R, m=P)
     out_halves = out.rearrange("h (k m r) e -> m h k (r e)", r=R, m=P)
@@ -37,23 +37,30 @@ def tile_rows_read_sig_norm_gate_kernel(tc, q, qa, S, og, out):
         ctx.enter_context(tc.manual_schedule())
 
         qa_t = sb.tile([P, PACK], F32, name="qa_t")
+        q_features = {}
         q_raw, phi, q_bf, q_codes, q_scales = {}, {}, {}, {}, {}
         s_raw, s_bf, s_codes, s_scales = {}, {}, {}, {}
         og_raw, gate, acc, rec, result, divided = {}, {}, {}, {}, {}, {}
 
-        def load_qa():
+        def load_qa(queue):
             for c in range(SIDE):
-                nc.scalar.dma_start(out=qa_t[ROWS * c : ROWS * (c + 1), :], in_=qa_rows)
+                queue.dma_start(out=qa_t[ROWS * c : ROWS * (c + 1), :], in_=qa_rows)
 
-        def load_q(u, m0, m1):
-            g, k = divmod(u, K)
-            raw = sb.tile([P, PACK, R * (m1 - m0)], F32, name="q_raw_%d_%d" % (u, m0), align_bytes=DMA_ALIGN)
-            nc.sync.dma_start(out=raw[:], in_=q_rows[P * g : P * (g + 1), :, W * k + R * m0 : W * k + R * m1])
-            q_raw[u, m0] = raw
+        def load_q(g, n0, n1):
+            raw = sb.tile([P, PACK, n1 - n0], F32, name="q_raw_%d_%d" % (g, n0), align_bytes=DMA_ALIGN)
+            nc.sync.dma_start(out=raw[:], in_=q_rows[P * g : P * (g + 1), :, n0:n1])
+            q_raw[g, n0] = raw
 
-        def load_s(g):
-            s_raw[g] = sb.tile([P, PACK, E], F32, name="s_raw_%d" % g, align_bytes=DMA_ALIGN)
-            nc.sync.dma_start(out=s_raw[g][:], in_=s_rows[P * g : P * (g + 1), :, :])
+        def load_q_features(g, n0, n1, a):
+            raw = sb.tile([P, 2, n1 - n0], F32, name="q_raw_%d_%d_%d" % (g, n0, a), align_bytes=DMA_ALIGN)
+            nc.sync.dma_start(out=raw[:], in_=q_rows[P * g : P * (g + 1), 2 * a : 2 * a + 2, n0:n1])
+            q_features[g, n0, a] = raw
+
+        def load_s(pairs):
+            raw = sb.tile([P, len(pairs), PACK * E], F32, name="s_raw_%d" % pairs[0], align_bytes=DMA_ALIGN)
+            nc.sync.dma_start(out=raw[:], in_=s_rows[:, pairs[0] : pairs[-1] + 1, :])
+            for i, g in enumerate(pairs):
+                s_raw[g] = raw[:, i, :].rearrange("p (j e) -> p j e", j=PACK)
 
         def load_og(heads, parts):
             raw = sb.tile(
@@ -67,10 +74,24 @@ def tile_rows_read_sig_norm_gate_kernel(tc, q, qa, S, og, out):
         def sigmoid_q(u, m0, m1):
             if u not in phi:
                 phi[u] = sb.tile([P, 2, W, 2], F32, name="phi_%d" % u)
-            first = max(m for v, m in q_raw if v == u and m <= m0)
+            g, k = divmod(u, K)
+            n0, n1 = W * k + R * m0, W * k + R * m1
+            first = max(n for pair, n in q_raw if pair == g and n <= n0)
             nc.scalar.activation(
                 out=phi[u][:, :, R * m0 : R * m1, :],
-                in_=q_raw[u, first][:, :, R * (m0 - first) : R * (m1 - first)].rearrange("p (a b) n -> p a n b", b=2),
+                in_=q_raw[g, first][:, :, n0 - first : n1 - first].rearrange("p (a b) n -> p a n b", b=2),
+                func=ACT.Sigmoid,
+            )
+
+        def sigmoid_q_features(u, m0, m1, a):
+            if u not in phi:
+                phi[u] = sb.tile([P, 2, W, 2], F32, name="phi_%d" % u)
+            g, k = divmod(u, K)
+            n0, n1 = W * k + R * m0, W * k + R * m1
+            first = max(n for pair, n, f in q_features if pair == g and f == a and n <= n0)
+            nc.scalar.activation(
+                out=phi[u][:, a, R * m0 : R * m1, :],
+                in_=q_features[g, first, a][:, :, n0 - first : n1 - first].rearrange("p b n -> p n b"),
                 func=ACT.Sigmoid,
             )
 
@@ -82,11 +103,18 @@ def tile_rows_read_sig_norm_gate_kernel(tc, q, qa, S, og, out):
                 for n, k in enumerate(parts):
                     gate[h, k] = gates[:, i, n, :]
 
+        def sigmoid_og_tile(h, k, r):
+            raw, i, n = og_raw[h, k]
+            if (h, k) not in gate:
+                gates = sb.tile([P, R * E], F32, name="gate_%d_%d" % (h, k))
+                gate[h, k] = gates[:]
+            nc.scalar.activation(out=gate[h, k][:, E * r : E * (r + 1)], in_=raw[:, i, n, E * r : E * (r + 1)], func=ACT.Sigmoid)
+
         def s_views(g):
             s_bf[g] = sb.tile([P, E, PACK], BF16, name="s_bf_%d" % g, align_bytes=64)
             return (
                 s_bf[g][:].rearrange("p (c i) j -> p c j i", i=4),
-                s_raw[g][:].rearrange("p j (c i) -> p c j i", i=4),
+                s_raw[g].rearrange("p j (c i) -> p c j i", i=4),
             )
 
         def round_s_on_scalar(g):
@@ -101,7 +129,7 @@ def tile_rows_read_sig_norm_gate_kernel(tc, q, qa, S, og, out):
             s_bf[g] = sb.tile([P, E, PACK], BF16, name="s_bf_%d" % g, align_bytes=64)
             nc.gpsimd.tensor_scalar(
                 out=s_bf[g][:],
-                in0=s_raw[g][:].rearrange("p j e -> p e j"),
+                in0=s_raw[g].rearrange("p j e -> p e j"),
                 scalar1=1.0,
                 scalar2=0.0,
                 op0=ALU.mult,
@@ -117,25 +145,39 @@ def tile_rows_read_sig_norm_gate_kernel(tc, q, qa, S, og, out):
                 in_=s_bf[g][:].rearrange("p e j -> p (e j)"),
             )
 
-        def weigh(u, m0, m1):
+        def weigh(u, m0, m1, engine=nc.vector):
             if u not in q_bf:
                 q_bf[u] = sb.tile([P, R, P, PACK], BF16, name="q_bf_%d" % u, align_bytes=DMA_ALIGN)
             qa_pairs = qa_t[:].rearrange("p (a b) -> p a b", b=2)
-            nc.vector.tensor_tensor(
+            engine.tensor_tensor(
                 out=q_bf[u][:, :, m0:m1, :].rearrange("p r m (a b) -> p m r a b", b=2),
                 in0=phi[u][:, :, R * m0 : R * m1, :].rearrange("p a (m r) b -> p m r a b", r=R),
                 in1=qa_pairs.unsqueeze(1).unsqueeze(1).to_broadcast([P, m1 - m0, R, 2, 2]),
                 op=ALU.mult,
             )
 
+        def quant_tiles(u):
+            if u not in q_codes:
+                q_codes[u] = sb.tile([P, R, P], U32, name="q_codes_%d" % u, align_bytes=64)
+                q_scales[u] = sb.tile([P, R, P], U8, name="q_scales_%d" % u, align_bytes=64)
+            return q_codes[u], q_scales[u]
+
         def quant_q(u):
-            q_codes[u] = sb.tile([P, R, P], U32, name="q_codes_%d" % u, align_bytes=64)
-            q_scales[u] = sb.tile([P, R, P], U8, name="q_scales_%d" % u, align_bytes=64)
+            codes, scales = quant_tiles(u)
             nc.vector.quantize_mx(
-                out=q_codes[u][:].rearrange("p r m -> p (r m)").bitcast(FP8X4),
-                scales=q_scales[u][:].rearrange("p r m -> p (r m)"),
+                out=codes[:].rearrange("p r m -> p (r m)").bitcast(FP8X4),
+                scales=scales[:].rearrange("p r m -> p (r m)"),
                 in_=q_bf[u][:].rearrange("p r m j -> p (r m j)"),
             )
+
+        def quant_q_columns(u, m0, m1):
+            codes, scales = quant_tiles(u)
+            for r in range(R):
+                nc.vector.quantize_mx(
+                    out=codes[:, r, m0:m1].bitcast(FP8X4),
+                    scales=scales[:, r, m0:m1],
+                    in_=q_bf[u][:, r, m0:m1, :].rearrange("p m j -> p (m j)"),
+                )
 
         def bank(name, halves):
             sums = ps.tile([P, len(halves), R, E], F32, name=name)
@@ -177,9 +219,9 @@ def tile_rows_read_sig_norm_gate_kernel(tc, q, qa, S, og, out):
             both, i, n = result[h, k]
             return both[:, i, n, :]
 
-        def store(heads, parts):
+        def store(heads, parts, queue=nc.sync):
             both, i0, n0 = result[heads[0], parts[0]]
-            nc.sync.dma_start(
+            queue.dma_start(
                 out=out_halves[:, heads[0] : heads[-1] + 1, parts[0] : parts[-1] + 1, :],
                 in_=both[:, i0 : i0 + len(heads), n0 : n0 + len(parts), :],
             )
@@ -200,10 +242,11 @@ def tile_rows_read_sig_norm_gate_kernel(tc, q, qa, S, og, out):
             for r in range(R):
                 finish_tile(h, k, r)
 
-        def divide(h, k):
+        def divide(h, k, tiles=range(R)):
             sums, i = acc[h, k]
-            divided[h, k] = sb.tile([P, R * E], F32, name="divided_%d_%d" % (h, k))
-            for r in range(R):
+            if (h, k) not in divided:
+                divided[h, k] = sb.tile([P, R * E], F32, name="divided_%d_%d" % (h, k))
+            for r in tiles:
                 nc.scalar.activation(
                     out=divided[h, k][:, E * r : E * (r + 1)],
                     in_=sums[:, i, r, :],
@@ -211,28 +254,27 @@ def tile_rows_read_sig_norm_gate_kernel(tc, q, qa, S, og, out):
                     scale=rec[h, k][:, r : r + 1],
                 )
 
-        def apply_gate(h, k):
-            nc.gpsimd.tensor_tensor(out=result_of(h, k), in0=divided[h, k][:], in1=gate[h, k], op=ALU.mult)
+        def apply_gate(h, k, tiles=range(R)):
+            cols = slice(E * tiles[0], E * (tiles[-1] + 1))
+            nc.gpsimd.tensor_tensor(out=result_of(h, k)[:, cols], in0=divided[h, k][:, cols], in1=gate[h, k][:, cols], op=ALU.mult)
 
         in_turn = [(c, r) for r in range(R) for c in range(SIDE)]
-
-        for h in (0, 2, 3):
+        by_head = [(c, r) for c in range(SIDE) for r in range(R)]
+        for h in range(4):
             bank("acc_%d" % h, [(h, 0), (h, 1)])
-        for k in range(K):
-            bank("acc_1_%d" % k, [(1, k)])
-        load_qa()
-        for u in (0, 1, 2):
-            load_q(u, 0, 64)
-            load_q(u, 64, 128)
-        load_s(0)
-        load_q(3, 0, 64)
-        load_q(3, 64, 128)
-        load_s(1)
+        load_qa(nc.scalar)
+        for n0 in range(0, 512, 128):
+            load_q(0, n0, n0 + 128)
+        load_q(1, 0, 128)
+        load_q(1, 128, 256)
+        load_s([0])
+        load_q(1, 256, 384)
+        load_q(1, 384, 512)
+        load_s([1])
         load_og([0, 1], [0])
         load_og([0, 1], [1])
         load_og([2], [0, 1])
         load_og([3], [0, 1])
-
         for m0 in range(0, 128, 32):
             sigmoid_q(0, m0, m0 + 32)
         sigmoid_q(1, 0, 32)
@@ -245,7 +287,6 @@ def tile_rows_read_sig_norm_gate_kernel(tc, q, qa, S, og, out):
         sigmoid_q(3, 64, 128)
         round_s_on_scalar(1)
         sigmoid_og([0, 1], [0])
-
         for m0 in range(0, 128, 32):
             weigh(0, m0, m0 + 32)
         weigh(1, 0, 32)
@@ -263,29 +304,28 @@ def tile_rows_read_sig_norm_gate_kernel(tc, q, qa, S, og, out):
         weigh(3, 64, 128)
         quant_s(1)
         products(2, in_turn)
-        inverse([(1, 0)])
         inverse([(0, 0), (0, 1)])
+        inverse([(1, 0), (1, 1)])
         quant_q(3)
-        inverse([(1, 1)])
-        products(3, [(0, 0), (0, 1), (1, 0), (1, 1)])
+        products(3, by_head)
         sigmoid_og([0], [1])
         sigmoid_og([1], [1])
-        divide(1, 0)
-        apply_gate(1, 0)
         for h in (2, 3):
             for k in range(K):
                 sigmoid_og([h], [k])
         finish(0, 0)
         store([0], [0])
+        finish(1, 0)
+        store([1], [0])
         finish(0, 1)
         store([0], [1])
-        finish(1, 1)
-        store([1], [1])
+        finish_tile(1, 1, 0)
         inverse([(2, 0), (2, 1)])
+        finish_tile(1, 1, 1)
+        store([1], [1])
         inverse([(3, 0), (3, 1)])
         finish(2, 0)
         store([2], [0])
-        store([1], [0])
         finish(2, 1)
         store([2], [1])
         for k in range(K):

from contextlib import ExitStack

import concourse.mybir as mybir

H, D, N, E = 4, 256, 512, 128
FLOPS = 2 * H * N * D * E

F32 = mybir.dt.float32
BF16 = mybir.dt.bfloat16
U32 = mybir.dt.uint32
U8 = mybir.dt.uint8
FP8X4 = mybir.dt.float8_e4m3fn_x4
ACT = mybir.ActivationFunctionType
ALU = mybir.AluOpType

P = 128
PACK = 4
ROWS = D // PACK
SIDE = P // ROWS
R = 2
W = P * R
K = N // W
DMA_ALIGN = 256


def tile_rows_read_sig_norm_gate_kernel(tc, q, qa, S, og, out):
    nc = tc.nc
    q_rows = q.rearrange("h (p j) n -> (h p) j n", j=PACK)
    s_rows = S.rearrange("(g c) (p j) e -> (c p) g (j e)", c=SIDE, j=PACK)
    qa_rows = qa.rearrange("(p j) o -> p (j o)", j=PACK)
    og_halves = og.rearrange("h (k m r) e -> m h k (r e)", r=R, m=P)
    out_halves = out.rearrange("h (k m r) e -> m h k (r e)", r=R, m=P)

    with ExitStack() as ctx:
        sb = ctx.enter_context(tc.tile_pool(name="sb", bufs=1))
        ps = ctx.enter_context(tc.psum_pool(name="ps", bufs=1))
        ctx.enter_context(tc.manual_schedule())

        qa_t = sb.tile([P, PACK], F32, name="qa_t")
        q_features = {}
        q_raw, phi, q_bf, q_codes, q_scales = {}, {}, {}, {}, {}
        s_raw, s_bf, s_codes, s_scales = {}, {}, {}, {}
        og_raw, gate, acc, rec, result, divided = {}, {}, {}, {}, {}, {}

        def load_qa(queue):
            for c in range(SIDE):
                queue.dma_start(out=qa_t[ROWS * c : ROWS * (c + 1), :], in_=qa_rows)

        def load_q(g, n0, n1):
            raw = sb.tile([P, PACK, n1 - n0], F32, name="q_raw_%d_%d" % (g, n0), align_bytes=DMA_ALIGN)
            nc.sync.dma_start(out=raw[:], in_=q_rows[P * g : P * (g + 1), :, n0:n1])
            q_raw[g, n0] = raw

        def load_q_features(g, n0, n1, a):
            raw = sb.tile([P, 2, n1 - n0], F32, name="q_raw_%d_%d_%d" % (g, n0, a), align_bytes=DMA_ALIGN)
            nc.sync.dma_start(out=raw[:], in_=q_rows[P * g : P * (g + 1), 2 * a : 2 * a + 2, n0:n1])
            q_features[g, n0, a] = raw

        def load_s(pairs):
            raw = sb.tile([P, len(pairs), PACK * E], F32, name="s_raw_%d" % pairs[0], align_bytes=DMA_ALIGN)
            nc.sync.dma_start(out=raw[:], in_=s_rows[:, pairs[0] : pairs[-1] + 1, :])
            for i, g in enumerate(pairs):
                s_raw[g] = raw[:, i, :].rearrange("p (j e) -> p j e", j=PACK)

        def load_og(heads, parts):
            raw = sb.tile(
                [P, len(heads), len(parts), R * E], F32, name="og_%d_%d" % (heads[0], parts[0]), align_bytes=DMA_ALIGN
            )
            nc.sync.dma_start(out=raw[:], in_=og_halves[:, heads[0] : heads[-1] + 1, parts[0] : parts[-1] + 1, :])
            for i, h in enumerate(heads):
                for n, k in enumerate(parts):
                    og_raw[h, k] = (raw, i, n)

        def sigmoid_q(u, m0, m1):
            if u not in phi:
                phi[u] = sb.tile([P, 2, W, 2], F32, name="phi_%d" % u)
            g, k = divmod(u, K)
            n0, n1 = W * k + R * m0, W * k + R * m1
            first = max(n for pair, n in q_raw if pair == g and n <= n0)
            nc.scalar.activation(
                out=phi[u][:, :, R * m0 : R * m1, :],
                in_=q_raw[g, first][:, :, n0 - first : n1 - first].rearrange("p (a b) n -> p a n b", b=2),
                func=ACT.Sigmoid,
            )

        def sigmoid_q_features(u, m0, m1, a):
            if u not in phi:
                phi[u] = sb.tile([P, 2, W, 2], F32, name="phi_%d" % u)
            g, k = divmod(u, K)
            n0, n1 = W * k + R * m0, W * k + R * m1
            first = max(n for pair, n, f in q_features if pair == g and f == a and n <= n0)
            nc.scalar.activation(
                out=phi[u][:, a, R * m0 : R * m1, :],
                in_=q_features[g, first, a][:, :, n0 - first : n1 - first].rearrange("p b n -> p n b"),
                func=ACT.Sigmoid,
            )

        def sigmoid_og(heads, parts):
            raw, i0, n0 = og_raw[heads[0], parts[0]]
            gates = sb.tile([P, len(heads), len(parts), R * E], F32, name="gate_%d_%d" % (heads[0], parts[0]))
            nc.scalar.activation(out=gates[:], in_=raw[:, i0 : i0 + len(heads), n0 : n0 + len(parts), :], func=ACT.Sigmoid)
            for i, h in enumerate(heads):
                for n, k in enumerate(parts):
                    gate[h, k] = gates[:, i, n, :]

        def sigmoid_og_tile(h, k, r):
            raw, i, n = og_raw[h, k]
            if (h, k) not in gate:
                gates = sb.tile([P, R * E], F32, name="gate_%d_%d" % (h, k))
                gate[h, k] = gates[:]
            nc.scalar.activation(out=gate[h, k][:, E * r : E * (r + 1)], in_=raw[:, i, n, E * r : E * (r + 1)], func=ACT.Sigmoid)

        def s_views(g):
            s_bf[g] = sb.tile([P, E, PACK], BF16, name="s_bf_%d" % g, align_bytes=64)
            return (
                s_bf[g][:].rearrange("p (c i) j -> p c j i", i=4),
                s_raw[g].rearrange("p j (c i) -> p c j i", i=4),
            )

        def round_s_on_scalar(g):
            dst, src = s_views(g)
            nc.scalar.copy(out=dst, in_=src)

        def round_s_on_vector(g):
            dst, src = s_views(g)
            nc.vector.tensor_copy(out=dst, in_=src)

        def round_s_on_gpsimd(g):
            s_bf[g] = sb.tile([P, E, PACK], BF16, name="s_bf_%d" % g, align_bytes=64)
            nc.gpsimd.tensor_scalar(
                out=s_bf[g][:],
                in0=s_raw[g].rearrange("p j e -> p e j"),
                scalar1=1.0,
                scalar2=0.0,
                op0=ALU.mult,
                op1=ALU.add,
            )

        def quant_s(g):
            s_codes[g] = sb.tile([P, E], U32, name="s_codes_%d" % g, align_bytes=64)
            s_scales[g] = sb.tile([P, E], U8, name="s_scales_%d" % g, align_bytes=64)
            nc.vector.quantize_mx(
                out=s_codes[g][:].bitcast(FP8X4),
                scales=s_scales[g][:],
                in_=s_bf[g][:].rearrange("p e j -> p (e j)"),
            )

        def weigh(u, m0, m1, engine=nc.vector):
            if u not in q_bf:
                q_bf[u] = sb.tile([P, R, P, PACK], BF16, name="q_bf_%d" % u, align_bytes=DMA_ALIGN)
            qa_pairs = qa_t[:].rearrange("p (a b) -> p a b", b=2)
            engine.tensor_tensor(
                out=q_bf[u][:, :, m0:m1, :].rearrange("p r m (a b) -> p m r a b", b=2),
                in0=phi[u][:, :, R * m0 : R * m1, :].rearrange("p a (m r) b -> p m r a b", r=R),
                in1=qa_pairs.unsqueeze(1).unsqueeze(1).to_broadcast([P, m1 - m0, R, 2, 2]),
                op=ALU.mult,
            )

        def quant_tiles(u):
            if u not in q_codes:
                q_codes[u] = sb.tile([P, R, P], U32, name="q_codes_%d" % u, align_bytes=64)
                q_scales[u] = sb.tile([P, R, P], U8, name="q_scales_%d" % u, align_bytes=64)
            return q_codes[u], q_scales[u]

        def quant_q(u):
            codes, scales = quant_tiles(u)
            nc.vector.quantize_mx(
                out=codes[:].rearrange("p r m -> p (r m)").bitcast(FP8X4),
                scales=scales[:].rearrange("p r m -> p (r m)"),
                in_=q_bf[u][:].rearrange("p r m j -> p (r m j)"),
            )

        def quant_q_columns(u, m0, m1):
            codes, scales = quant_tiles(u)
            for r in range(R):
                nc.vector.quantize_mx(
                    out=codes[:, r, m0:m1].bitcast(FP8X4),
                    scales=scales[:, r, m0:m1],
                    in_=q_bf[u][:, r, m0:m1, :].rearrange("p m j -> p (m j)"),
                )

        def bank(name, halves):
            sums = ps.tile([P, len(halves), R, E], F32, name=name)
            for i, half in enumerate(halves):
                acc[half] = (sums, i)

        def products(u, tiles):
            g, k = divmod(u, K)
            for c, r in tiles:
                sums, i = acc[SIDE * g + c, k]
                rows = slice(ROWS * c, ROWS * (c + 1))
                nc.tensor.matmul_mx(
                    out=sums[:, i, r, :],
                    lhsT=q_codes[u][rows, r, :].bitcast(FP8X4),
                    lhsT_scale=q_scales[u][rows, r, :],
                    rhs=s_codes[g][rows, :].bitcast(FP8X4),
                    rhs_scale=s_scales[g][rows, :],
                    start=True,
                    stop=True,
                )

        def inverse(halves):
            sums, i0 = acc[halves[0]]
            inv = sb.tile([P, len(halves), R], F32, name="rec_%d_%d" % halves[0])
            nc.vector.reciprocal(out=inv[:], in_=sums[:, i0 : i0 + len(halves), :, E - 1])
            for i, half in enumerate(halves):
                rec[half] = inv[:, i, :]

        def results(heads, parts, tag=None):
            name = "result_%d_%d" % (heads[0], parts[0])
            both = sb.tile([P, len(heads), len(parts), R * E], F32, name=name, tag=tag or name, align_bytes=DMA_ALIGN)
            for i, h in enumerate(heads):
                for n, k in enumerate(parts):
                    result[h, k] = (both, i, n)

        def result_of(h, k):
            if (h, k) not in result:
                results([h], [k])
            both, i, n = result[h, k]
            return both[:, i, n, :]

        def store(heads, parts, queue=nc.sync):
            both, i0, n0 = result[heads[0], parts[0]]
            queue.dma_start(
                out=out_halves[:, heads[0] : heads[-1] + 1, parts[0] : parts[-1] + 1, :],
                in_=both[:, i0 : i0 + len(heads), n0 : n0 + len(parts), :],
            )

        def finish_tile(h, k, r):
            cols = slice(E * r, E * (r + 1))
            sums, i = acc[h, k]
            nc.vector.scalar_tensor_tensor(
                out=result_of(h, k)[:, cols],
                in0=sums[:, i, r, :],
                scalar=rec[h, k][:, r : r + 1],
                in1=gate[h, k][:, cols],
                op0=ALU.mult,
                op1=ALU.mult,
            )

        def finish(h, k):
            for r in range(R):
                finish_tile(h, k, r)

        def divide(h, k, tiles=range(R)):
            sums, i = acc[h, k]
            if (h, k) not in divided:
                divided[h, k] = sb.tile([P, R * E], F32, name="divided_%d_%d" % (h, k))
            for r in tiles:
                nc.scalar.activation(
                    out=divided[h, k][:, E * r : E * (r + 1)],
                    in_=sums[:, i, r, :],
                    func=ACT.Copy,
                    scale=rec[h, k][:, r : r + 1],
                )

        def apply_gate(h, k, tiles=range(R)):
            cols = slice(E * tiles[0], E * (tiles[-1] + 1))
            nc.gpsimd.tensor_tensor(out=result_of(h, k)[:, cols], in0=divided[h, k][:, cols], in1=gate[h, k][:, cols], op=ALU.mult)

        in_turn = [(c, r) for r in range(R) for c in range(SIDE)]
        by_head = [(c, r) for c in range(SIDE) for r in range(R)]
        for h in range(4):
            bank("acc_%d" % h, [(h, 0), (h, 1)])
        load_qa(nc.scalar)
        for n0 in range(0, 512, 128):
            load_q(0, n0, n0 + 128)
        load_q(1, 0, 128)
        load_q(1, 128, 256)
        load_s([0])
        load_q(1, 256, 384)
        load_q(1, 384, 512)
        load_s([1])
        load_og([0, 1], [0])
        load_og([0, 1], [1])
        load_og([2], [0, 1])
        load_og([3], [0, 1])
        for m0 in range(0, 128, 32):
            sigmoid_q(0, m0, m0 + 32)
        sigmoid_q(1, 0, 32)
        sigmoid_q(1, 32, 64)
        sigmoid_q(1, 64, 128)
        sigmoid_q(2, 0, 64)
        sigmoid_q(2, 64, 128)
        round_s_on_scalar(0)
        sigmoid_q(3, 0, 64)
        sigmoid_q(3, 64, 128)
        round_s_on_scalar(1)
        sigmoid_og([0, 1], [0])
        for m0 in range(0, 128, 32):
            weigh(0, m0, m0 + 32)
        weigh(1, 0, 32)
        weigh(1, 32, 64)
        quant_q(0)
        weigh(1, 64, 128)
        weigh(2, 0, 64)
        weigh(2, 64, 128)
        quant_q(1)
        quant_s(0)
        products(0, in_turn)
        products(1, in_turn)
        quant_q(2)
        weigh(3, 0, 64)
        weigh(3, 64, 128)
        quant_s(1)
        products(2, in_turn)
        inverse([(0, 0), (0, 1)])
        inverse([(1, 0), (1, 1)])
        quant_q(3)
        products(3, by_head)
        sigmoid_og([0], [1])
        sigmoid_og([1], [1])
        for h in (2, 3):
            for k in range(K):
                sigmoid_og([h], [k])
        finish(0, 0)
        store([0], [0])
        finish(1, 0)
        store([1], [0])
        finish(0, 1)
        store([0], [1])
        finish_tile(1, 1, 0)
        inverse([(2, 0), (2, 1)])
        finish_tile(1, 1, 1)
        store([1], [1])
        inverse([(3, 0), (3, 1)])
        finish(2, 0)
        store([2], [0])
        finish(2, 1)
        store([2], [1])
        for k in range(K):
            finish(3, k)
            store([3], [k])
